import numpy as np
import ml_dtypes


def mxq(x, axis, fmt="e4m3"):
    dtype, down = {"e4m3": (ml_dtypes.float8_e4m3fn, 7), "e5m2": (ml_dtypes.float8_e5m2, 14)}[fmt]
    v = np.moveaxis(np.asarray(x, np.float32).astype(ml_dtypes.bfloat16).astype(np.float64), axis, -1)
    blocks = v.reshape(v.shape[:-1] + (-1, 32))
    amax = np.abs(blocks).max(-1, keepdims=True)
    byte = np.maximum(np.where(amax > 0, np.frexp(amax)[1] - 1 + 127, 0) - down, 1)
    scale = np.exp2(byte - 127.0)
    codes = (blocks / scale).astype(np.float32).astype(dtype).astype(np.float64)
    return np.moveaxis((codes * scale).reshape(v.shape), -1, axis)


WIDE = False


def mx_kscale(k):
    if not WIDE:
        return np.ones(k)
    levels = np.array([10, -10, 5, -5, 0])
    if k % 512:
        return np.exp2(np.random.permutation(np.resize(levels, k // 32))).repeat(32)
    a = np.empty((k // 512, 16))
    for p in range(k // 512):
        a[p, :8] = np.random.permutation(np.resize(levels, 8))
        for g in range(8):
            far = levels[np.abs(levels - a[p, g]) >= 10]
            a[p, g + 8] = far[np.random.randint(len(far))]
    return np.exp2(a.ravel()).repeat(32)


def f64(x):
    return np.asarray(x).astype(np.float64)


def striped8(idx):
    return np.asarray(idx).reshape(8, -1, 16).transpose(0, 2, 1).reshape(128, -1).astype(np.uint16)


def unstriped8(offs):
    return offs.reshape(8, 16, -1).transpose(0, 2, 1).reshape(8, -1).astype(np.int64)


def pick8(x, idx, run):
    r = np.arange(len(x))
    return x[r[:, None], idx[r % (8 * run) // run]]


def sigmoid(v):
    return 1.0 / (1.0 + np.exp(-v))


def bf(x):
    return np.asarray(x, np.float32).astype(ml_dtypes.bfloat16)


def planes(Y):
    r, m = Y.shape
    b = f64(bf(Y)).reshape(r // 32, 32, m)
    amax = np.abs(b).max(1)
    byte = np.clip(np.where(amax > 0, np.frexp(amax)[1] - 1 + 127 - 7, 1), 1, 254)
    codes = (b * np.exp2(127.0 - byte)[:, None, :]).reshape(r, m).astype(np.float32).astype(ml_dtypes.float8_e4m3fn).view(np.uint8)
    words = codes.reshape(r // 512, 128, 4, m).transpose(0, 1, 3, 2)
    return np.ascontiguousarray(words), np.ascontiguousarray(byte.astype(np.uint8).reshape(r // 512, 16, m))


D, T, I, Q, X, E, K = 512, 1024, 512, 512, 64, 512, 512


def setup_inputs():
    n = np.random.standard_normal
    idx = np.stack([np.random.permutation(T)[:I] for _ in range(8)])
    fd = mx_kscale(D)
    fi = mx_kscale(I)
    fk = mx_kscale(K)
    ti = np.ones((8, T))
    np.put_along_axis(ti, idx, np.tile(fi, (8, 1)), axis=1)
    return {
        "query": (n((D, Q)) * (np.arange(D)[:, None] // 64 == np.arange(Q) % 8) * 0.0625 * fd[:, None]).astype(np.float32),
        "keys": (n((D, T)) / fd[:, None]).astype(np.float32),
        "size": (np.random.uniform(0.5, 2.0, (1, I)) * fi).astype(np.float32),
        "vals": (n((E, T)) / ti[np.arange(E) % 512 // 64]).astype(np.float32),
        "own": ((np.arange(E)[:, None] // 64 == np.arange(Q) % 8) * 1.0).astype(np.float32),
        "inp": (n((K, X)) * fk[:, None]).astype(np.float32),
        "wg": (n((K, E)) * 1 / np.sqrt(K) / fk[:, None]).astype(np.float32),
        "offs": striped8(idx),
    }


def reference(query, keys, size, vals, own, inp, wg, offs):
    idx = unstriped8(offs)
    queryq = mxq(f64(query), 0, "e4m3")
    keysidxq = mxq(pick8(f64(keys), idx, 64), 0, "e4m3")
    a = queryq.T @ keysidxq
    p = np.exp(a - np.max(a, axis=1, keepdims=True))
    w = p * f64(size) / np.sum(p, axis=1, keepdims=True)
    wt = w.T
    vt = pick8(f64(vals), idx, 64).T
    vtq = mxq(vt, 0, "e4m3")
    wtq = mxq(wt, 0, "e4m3")
    o = vtq.T @ wtq
    ob = o * f64(own)
    wgq = mxq(f64(wg), 0, "e4m3")
    inpq = mxq(f64(inp), 0, "e4m3")
    g = wgq.T @ inpq
    y = ob.reshape(E, X, Q // X).sum(axis=2) * sigmoid(g)
    words, scales = planes(y)
    return y, words, scales

@@ -1,0 +1,238 @@
+from contextlib import ExitStack
+
+import concourse.mybir as mybir
+from concourse.masks import make_identity
+
+D, T, I, Q, X, E, K = 512, 1024, 512, 512, 64, 512, 512
+FLOPS = 2 * D * Q * I + 2 * I * E * Q + 2 * K * E * X
+
+F32 = mybir.dt.float32
+BF16 = mybir.dt.bfloat16
+I32 = mybir.dt.int32
+U32 = mybir.dt.uint32
+U16 = mybir.dt.uint16
+U8 = mybir.dt.uint8
+FP8X4 = mybir.dt.float8_e4m3fn_x4
+ALU = mybir.AluOpType
+ACT = mybir.ActivationFunctionType
+AXIS = mybir.AxisListType
+
+P = 128
+PACK = 4
+HEADS = 8
+QT = Q // P
+XT = P // HEADS
+LOADS = ["k0","s","k1","k2","k3","q0","q1","p0","p1","v2","v3","i","w","o"]
+ORDER = ["q0","q1","e0","e1","v2","p0","w0","e2","w1","e3","v3","w2","w3","g0","o0","o1","o2","o3","s0","y0","y1"]
+KSPLIT = 512
+CASTN = 2
+WGN = 2
+OWNN = 1
+WG_ENG = "SSSS"
+Q_ENG = "SS"
+
+
+def tile_attend_ownlists_gate_pl_kernel(tc, query, keys, size, vals, own, inp, wg, offs, out_0, out_1, out_2):
+    nc = tc.nc
+    with ExitStack() as ctx:
+        sb = ctx.enter_context(tc.tile_pool(name="sb", bufs=1))
+        ps = ctx.enter_context(tc.psum_pool(name="ps", bufs=1))
+
+        def quantise(name, grouped, words):
+            codes = sb.tile([P, words], U32, name=name + "_codes", align_bytes=64)
+            scales = sb.tile([P, words], U8, name=name + "_scales", align_bytes=64)
+            nc.vector.quantize_mx(out=codes[:].bitcast(FP8X4), scales=scales[:], in_=grouped)
+            return codes, scales
+
+        def product(out, lhs, lcols, rhs):
+            nc.tensor.matmul_mx(out=out, lhsT=lhs[0][:, lcols].bitcast(FP8X4), lhsT_scale=lhs[1][:, lcols],
+                                rhs=rhs[0][:].bitcast(FP8X4), rhs_scale=rhs[1][:], start=True, stop=True)
+
+        def cast(eng, out, in_):
+            if eng == "S":
+                nc.scalar.copy(out, in_)
+            elif eng == "V":
+                nc.vector.tensor_copy(out, in_)
+            else:
+                nc.gpsimd.tensor_scalar(out, in_, 1.0, 0.0, ALU.mult, ALU.add)
+
+        offsets = sb.tile([P, I // 16], U16, name="offsets")
+        nc.sync.dma_start(offsets[:], offs)
+        keys_v = keys.rearrange("(p j) t -> j p t", j=PACK)
+        vals_v = vals.rearrange("(p j) t -> j p t", j=PACK)
+        query_v = query.rearrange("(p j) q -> p j q", j=PACK)
+        own_v = own.rearrange("(p j) q -> p j q", j=PACK)
+        wg_v = wg.rearrange("(p j) e -> p j e", j=PACK)
+        key_planes = [sb.tile([P, T], F32, name="key_plane%d" % j) for j in range(PACK)]
+        val_planes = [sb.tile([P, T], F32, name="val_plane%d" % j) for j in range(PACK)]
+        val_two = [sb.tile([P, 2, T // 2], F32, name="val_two%d" % j) for j in range(4)]
+        query_raw = [sb.tile([P, PACK, Q // 2], F32, name="query_raw%d" % h) for h in range(2)]
+        size4 = sb.tile([P, PACK], F32, name="size4")
+        own_sb = [sb.tile([P, PACK, Q // OWNN], F32, name="own_sb%d" % h) for h in range(OWNN)]
+        inp_raw = sb.tile([P, PACK, X], F32, name="inp_raw")
+        wg_raw = sb.tile([P, PACK, E], F32, name="wg_raw")
+        for name in LOADS:
+            n = int(name[1:] or "0")
+            if name[0] == "k":
+                nc.sync.dma_start(key_planes[n][:], keys_v[n])
+            elif name[0] == "s":
+                nc.sync.dma_start(size4[:], size.rearrange("o (s t) -> s (o t)", t=PACK))
+            elif name[0] == "q":
+                nc.sync.dma_start(query_raw[n][:], query_v[:, :, n * (Q // 2):(n + 1) * (Q // 2)])
+            elif name[0] == "v":
+                nc.sync.dma_start(val_planes[n][:], vals_v[n])
+            elif name[0] == "p":
+                nc.sync.dma_start(val_two[n][:], vals.rearrange("(p j) t -> p j t", j=PACK)[:, 2 * (n // 2):2 * (n // 2) + 2, (n % 2) * (T // 2):(n % 2 + 1) * (T // 2)])
+            elif name[0] == "o":
+                nc.sync.dma_start(own_sb[n][:], own_v[:, :, n * (Q // OWNN):(n + 1) * (Q // OWNN)])
+            elif name[0] == "i":
+                nc.sync.dma_start(inp_raw[:], inp.rearrange("(p j) x -> p j x", j=PACK))
+            elif name[0] == "w":
+                nc.sync.dma_start(wg_raw[:], wg_v)
+
+        ident = sb.tile([P, P], F32, name="ident")
+        make_identity(nc, ident[:])
+
+        size_ps = ps.tile([P, PACK, P], F32, name="size_ps", tag="o", bufs=3)
+        for t in range(PACK):
+            nc.tensor.transpose(size_ps[:, t, :], size4[:, t:t + 1].to_broadcast([P, P]), ident[:])
+        size_row = sb.tile([P, P, PACK], F32, name="size_row")
+        nc.scalar.activation(size_row[:], size_ps[:].rearrange("p t s -> p s t"), ACT.Copy)
+
+        keys_g = sb.tile([P, PACK, I], BF16, name="keys_g")
+        for j in range(PACK):
+            nc.vector.tensor_copy(keys_g[:, j, :], key_planes[j][:].indirect(offsets[:]))
+        keys_w = sb.tile([P, I * PACK], BF16, name="keys_w", align_bytes=64)
+        for eng, a, b in (("V", 0, KSPLIT), ("S", KSPLIT, I)):
+            if b > a:
+                cast(eng, keys_w[:, a * PACK:b * PACK].rearrange("p (c i t) -> p c t i", i=4, t=PACK),
+                     keys_g[:, :, a:b].rearrange("p t (c i) -> p c t i", i=4))
+        keys_q = quantise("keys", keys_w[:], I)
+
+        query_q = {}
+        w_q = {}
+        w_sb = {}
+        p_sb = {}
+        p_sum = {}
+        vals_q = {}
+        o_ps = {}
+        gate = {}
+        half_sum = sb.tile([P, PACK, X], F32, name="half_sum")
+        y = sb.tile([P, PACK, X], F32, name="y")
+        y_w = sb.tile([P, X * PACK], BF16, name="y_w", align_bytes=64)
+
+        ob_lo = sb.tile([P, PACK, 2 * P], F32, name="ob_lo")
+
+        def do_query(h):
+            query_w = sb.tile([P, Q // 2 * PACK], BF16, name="query_w%d" % h, align_bytes=64)
+            cast(Q_ENG[h], query_w[:].rearrange("p (c i t) -> p c t i", i=4, t=PACK),
+                 query_raw[h][:].rearrange("p t (c i) -> p c t i", i=4))
+            query_q[h] = quantise("query%d" % h, query_w[:], Q // 2)
+
+        def do_exp(b):
+            a_ps = ps.tile([P, I], F32, name="a_ps%d" % b, tag="scores", bufs=2)
+            product(a_ps[:], query_q[b // 2], slice((b % 2) * P, (b % 2 + 1) * P), keys_q)
+            neg_max = sb.tile([P, 1], F32, name="neg_max%d" % b)
+            nc.vector.tensor_reduce(neg_max[:], a_ps[:], AXIS.X, ALU.max, negate=True)
+            p_sb[b] = sb.tile([P, I], F32, name="p_sb%d" % b)
+            p_sum[b] = sb.tile([P, 1], F32, name="p_sum%d" % b)
+            nc.scalar.activation(p_sb[b][:], a_ps[:], ACT.Exp, bias=neg_max[:], accum_out=p_sum[b][:])
+
+        def do_weights(b):
+            p_inv = sb.tile([P, 1], F32, name="p_inv%d" % b)
+            nc.vector.reciprocal(p_inv[:], p_sum[b][:])
+            w_sb = sb.tile([P, I], BF16, name="w_sb%d" % b)
+            nc.vector.scalar_tensor_tensor(w_sb[:], p_sb[b][:], p_inv[:], size_row[:].rearrange("p s t -> p (s t)"),
+                                           ALU.mult, ALU.mult)
+            w_ps = ps.tile([P, 2, P], F32, name="w_ps%d" % b, tag="wturn", bufs=1)
+            for u in range(2):
+                nc.tensor.transpose(w_ps[:, u, :], w_sb[:].bitcast(F32)[:, u:I // 2:2], ident[:])
+            w_w = sb.tile([P, P * PACK], BF16, name="w_w%d" % b, align_bytes=64)
+            nc.scalar.copy(w_w[:].bitcast(F32).rearrange("p (q u) -> p q u", u=2), w_ps[:].rearrange("p u q -> p q u"))
+            w_q[b] = quantise("w%d" % b, w_w[:], P)
+
+        def do_vals(r):
+            vals_g = sb.tile([P, I], BF16, name="vals_g%d" % r)
+            nc.vector.tensor_copy(vals_g[:], val_planes[r][:].indirect(offsets[:]))
+            v_ps = ps.tile([P, 2, P], F32, name="v_ps%d" % r, tag="vturn", bufs=1)
+            for u in range(2):
+                nc.tensor.transpose(v_ps[:, u, :], vals_g[:].bitcast(F32)[:, u:I // 2:2], ident[:])
+            v_w = sb.tile([P, P * PACK], BF16, name="v_w%d" % r, align_bytes=64)
+            nc.scalar.copy(v_w[:].bitcast(F32).rearrange("p (m u) -> p m u", u=2), v_ps[:].rearrange("p u m -> p m u"))
+            vals_q[r] = (quantise("v%d" % r, v_w[:], P), slice(0, P))
+
+        def do_pair(n):
+            pairs = sb.tile([P, T, 2], BF16, name="pairs%d" % n)
+            w = T // CASTN
+            for c in range(CASTN):
+                nc.scalar.activation(pairs[:, c * w:(c + 1) * w, :].rearrange("p (c i) r -> p c r i", i=4),
+                                     val_two[2 * n + c][:].rearrange("p r (c i) -> p c r i", i=4), ACT.Copy)
+            pairs_g = sb.tile([P, I], U32, name="pairs_g%d" % n)
+            nc.vector.tensor_copy(pairs_g[:], pairs[:].rearrange("p t r -> p (t r)").bitcast(U32).indirect(offsets[:]))
+            v_ps = ps.tile([P, PACK, P], F32, name="vp_ps%d" % n, tag="vturn", bufs=1)
+            for t in range(PACK):
+                nc.tensor.transpose(v_ps[:, t, :], pairs_g[:].bitcast(F32)[:, t:I:PACK], ident[:])
+            v_w = sb.tile([P, 2 * P * PACK], BF16, name="vp_w%d" % n, align_bytes=64)
+            nc.scalar.copy(v_w[:].rearrange("p (r m t) -> p r m t", r=2, t=PACK),
+                           v_ps[:].bitcast(BF16).rearrange("p t (m r) -> p r m t", r=2))
+            both = quantise("vp%d" % n, v_w[:], 2 * P)
+            for r in range(2):
+                vals_q[2 * n + r] = (both, slice(r * P, (r + 1) * P))
+
+        def do_out(b):
+            o_ps = ps.tile([P, PACK, P], F32, name="o_ps%d" % b, tag="o", bufs=3)
+            for r in range(PACK):
+                product(o_ps[:, r, :], vals_q[r][0], vals_q[r][1], w_q[b])
+            if b < 2:
+                ob = ob_lo[:, :, b * P:(b + 1) * P]
+            else:
+                ob = sb.tile([P, PACK, P], F32, name="ob%d" % b)
+            w = Q // OWNN
+            nc.vector.scalar_tensor_tensor(ob[:], o_ps[:], 0.5, own_sb[b * P // w][:, :, b * P % w:b * P % w + P], ALU.mult, ALU.mult)
+            if b >= 2:
+                nc.vector.tensor_reduce(half_sum[:, :, b * XT:(b + 1) * XT],
+                                        ob[:].rearrange("p r (x j) -> p r x j", j=HEADS), AXIS.X, ALU.add)
+
+        def do_sum(n):
+            st_ps = ps.tile([P, P], F32, name="st_ps", tag="scores", bufs=2)
+            flat = ob_lo[:].rearrange("p r q -> p (r q)")
+            for j in range(HEADS):
+                nc.tensor.matmul(st_ps[:], lhsT=flat[:, j:PACK * 2 * P:HEADS], rhs=ident[:], start=(j == 0), stop=(j == HEADS - 1), is_transpose=True)
+            st_sb = sb.tile([P, P], F32, name="st_sb")
+            nc.scalar.copy(st_sb[:], st_ps[:])
+            gate[1] = ps.tile([P, P], F32, name="back_ps", tag="scores", bufs=2)
+            nc.tensor.transpose(gate[1][:], st_sb[:], ident[:])
+
+        def do_y(h):
+            cols = slice(h * X // 2, (h + 1) * X // 2)
+            src = half_sum[:, :, cols] if h else gate[1][:].rearrange("p (r x) -> p r x", r=PACK)
+            nc.vector.scalar_tensor_tensor(y[:, :, cols], gate[0][:, :, cols], 1.0, src, ALU.add, ALU.mult)
+            cast("V" if h else "S", y_w[:].rearrange("p (x r) -> p x r", r=PACK)[:, cols, :], y[:, :, cols].rearrange("p r x -> p x r"))
+
+        def do_gate(n):
+            inp_w = sb.tile([P, X * PACK], BF16, name="inp_w", align_bytes=64)
+            nc.scalar.copy(inp_w[:].rearrange("p (c i t) -> p c t i", i=4, t=PACK),
+                           inp_raw[:].rearrange("p t (c i) -> p c t i", i=4))
+            inp_q = quantise("inp", inp_w[:], X)
+            wg_w = sb.tile([P, E * PACK], BF16, name="wg_w", align_bytes=64)
+            w = P // WGN
+            for c in range(WGN):
+                cast(WG_ENG[c], wg_w[:].rearrange("p (r m t) -> p m t r", r=PACK, t=PACK)[:, c * w:(c + 1) * w],
+                     wg_raw[:].rearrange("p t (m r) -> p m t r", r=PACK)[:, c * w:(c + 1) * w])
+            wg_q = quantise("wg", wg_w[:], E)
+            g_ps = ps.tile([P, PACK, X], F32, name="g_ps", tag="g", bufs=1)
+            for r in range(PACK):
+                product(g_ps[:, r, :], wg_q, slice(r * P, (r + 1) * P), inp_q)
+            gate[0] = sb.tile([P, PACK, X], F32, name="g_tanh")
+            nc.scalar.activation(gate[0][:], g_ps[:], ACT.Tanh, scale=0.5)
+
+        steps = {"q": do_query, "e": do_exp, "w": do_weights, "v": do_vals, "p": do_pair, "o": do_out, "g": do_gate, "s": do_sum, "y": do_y}
+        for name in ORDER:
+            steps[name[0]](int(name[1:]))
+
+        nc.sync.dma_start(out_0.rearrange("(p r) x -> p r x", r=PACK), y[:])
+        y_codes, y_scales = quantise("y", y_w[:], X)
+        nc.sync.dma_start(out_1[0].rearrange("p c r -> p (c r)").bitcast(I32), y_codes[:].bitcast(I32))
+        for g in range(4):
+            eng = nc.scalar if g % 2 else nc.sync
+            eng.dma_start(out_2[0, 4 * g:4 * g + 4, :].bitcast(I32), y_scales[32 * g:32 * g + 4, :].bitcast(I32))

@@ -22,14 +22,16 @@ PACK = 4
 HEADS = 8
 QT = Q // P
 XT = P // HEADS
-LOADS = ["k0","s","k1","k2","k3","q0","q1","p0","p1","v2","v3","i","w","o"]
-ORDER = ["q0","q1","e0","e1","v2","p0","w0","e2","w1","e3","v3","w2","w3","g0","o0","o1","o2","o3","s0","y0","y1"]
+LOADS = ["k0","s","k1","k2","k3","q0","v0","q1","v1","w","v2","v3","i","o"]
+ORDER = ["qi0","qq0","sc0","sc1","vg0","qi1","mx0","ex0","mx1","ex1","qq1","sc2","sc3","gw0","gw1","gw2","gw3","vg1","rc0","rc1","we0","mx2","ex2","we1","mx3","ex3","vg2","vg3","rc2","wq0","we2","rc3","wq1","we3","vq0","vq2","vq3","om0","om1","om2","om3","om10","om11","om12","om13","gi0","iq0","gq0","wq2","wq3","om20","om21","om22","om23","om30","om31","om32","om33","ob0","su0","ob1","su1","ob2","ob3","rd2","rd3","ya0","yb0","ya1","yb1"]
+TAGS = {"vals_g0":"raw_q0","vals_g1":"raw_q1","vals_g2":"x2","w_sb0":"x2","vals_g3":"x3","w_sb1":"x3","v01_codes":"x4","p_sb2":"x4","wg_codes":"x5","v_w01":"x5"}
 KSPLIT = 512
-CASTN = 2
-WGN = 2
+WGN = 4
 OWNN = 1
 WG_ENG = "SSSS"
 Q_ENG = "SS"
+PE_R = [0,1]
+CUTS = [[0,512]]
 
 
 def tile_attend_ownlists_gate_pl_kernel(tc, query, keys, size, vals, own, inp, wg, offs, out_0, out_1, out_2):
@@ -38,9 +40,12 @@ def tile_attend_ownlists_gate_pl_kernel(tc, query, keys, size, vals, own, inp, w
         sb = ctx.enter_context(tc.tile_pool(name="sb", bufs=1))
         ps = ctx.enter_context(tc.psum_pool(name="ps", bufs=1))
 
+        def tile(shape, dtype, name):
+            return sb.tile(shape, dtype, name=name, tag=TAGS.get(name, name), align_bytes=64)
+
         def quantise(name, grouped, words):
-            codes = sb.tile([P, words], U32, name=name + "_codes", align_bytes=64)
-            scales = sb.tile([P, words], U8, name=name + "_scales", align_bytes=64)
+            codes = tile([P, words], U32, name + "_codes")
+            scales = tile([P, words], U8, name + "_scales")
             nc.vector.quantize_mx(out=codes[:].bitcast(FP8X4), scales=scales[:], in_=grouped)
             return codes, scales
 
@@ -63,176 +68,217 @@ def tile_attend_ownlists_gate_pl_kernel(tc, query, keys, size, vals, own, inp, w
         query_v = query.rearrange("(p j) q -> p j q", j=PACK)
         own_v = own.rearrange("(p j) q -> p j q", j=PACK)
         wg_v = wg.rearrange("(p j) e -> p j e", j=PACK)
-        key_planes = [sb.tile([P, T], F32, name="key_plane%d" % j) for j in range(PACK)]
-        val_planes = [sb.tile([P, T], F32, name="val_plane%d" % j) for j in range(PACK)]
-        val_two = [sb.tile([P, 2, T // 2], F32, name="val_two%d" % j) for j in range(4)]
-        query_raw = [sb.tile([P, PACK, Q // 2], F32, name="query_raw%d" % h) for h in range(2)]
-        size4 = sb.tile([P, PACK], F32, name="size4")
-        own_sb = [sb.tile([P, PACK, Q // OWNN], F32, name="own_sb%d" % h) for h in range(OWNN)]
-        inp_raw = sb.tile([P, PACK, X], F32, name="inp_raw")
-        wg_raw = sb.tile([P, PACK, E], F32, name="wg_raw")
+        raw = {}
         for name in LOADS:
             n = int(name[1:] or "0")
             if name[0] == "k":
-                nc.sync.dma_start(key_planes[n][:], keys_v[n])
+                shape, src = [P, T], keys_v[n]
             elif name[0] == "s":
-                nc.sync.dma_start(size4[:], size.rearrange("o (s t) -> s (o t)", t=PACK))
+                shape, src = [P, PACK], size.rearrange("o (s t) -> s (o t)", t=PACK)
             elif name[0] == "q":
-                nc.sync.dma_start(query_raw[n][:], query_v[:, :, n * (Q // 2):(n + 1) * (Q // 2)])
+                shape, src = [P, PACK, Q // 2], query_v[:, :, n * (Q // 2):(n + 1) * (Q // 2)]
             elif name[0] == "v":
-                nc.sync.dma_start(val_planes[n][:], vals_v[n])
+                shape, src = [P, T], vals_v[n]
             elif name[0] == "p":
-                nc.sync.dma_start(val_two[n][:], vals.rearrange("(p j) t -> p j t", j=PACK)[:, 2 * (n // 2):2 * (n // 2) + 2, (n % 2) * (T // 2):(n % 2 + 1) * (T // 2)])
+                shape, src = [P, 2, T // 2], vals.rearrange("(p j) t -> p j t", j=PACK)[:, 2 * (n // 2):2 * (n // 2) + 2, (n % 2) * (T // 2):(n % 2 + 1) * (T // 2)]
             elif name[0] == "o":
-                nc.sync.dma_start(own_sb[n][:], own_v[:, :, n * (Q // OWNN):(n + 1) * (Q // OWNN)])
+                shape, src = [P, PACK, Q // OWNN], own_v[:, :, n * (Q // OWNN):(n + 1) * (Q // OWNN)]
             elif name[0] == "i":
-                nc.sync.dma_start(inp_raw[:], inp.rearrange("(p j) x -> p j x", j=PACK))
-            elif name[0] == "w":
-                nc.sync.dma_start(wg_raw[:], wg_v)
+                shape, src = [P, PACK, X], inp.rearrange("(p j) x -> p j x", j=PACK)
+            else:
+                shape, src = [P, PACK, E], wg_v
+            raw[name] = tile(shape, F32, "raw_" + name)
+            nc.sync.dma_start(raw[name][:], src)
 
         ident = sb.tile([P, P], F32, name="ident")
         make_identity(nc, ident[:])
 
-        size_ps = ps.tile([P, PACK, P], F32, name="size_ps", tag="o", bufs=3)
+        size_ps = ps.tile([P, PACK, P], F32, name="size_ps", tag="misc", bufs=1)
         for t in range(PACK):
-            nc.tensor.transpose(size_ps[:, t, :], size4[:, t:t + 1].to_broadcast([P, P]), ident[:])
-        size_row = sb.tile([P, P, PACK], F32, name="size_row")
+            nc.tensor.transpose(size_ps[:, t, :], raw["s"][:, t:t + 1].to_broadcast([P, P]), ident[:])
+        size_row = tile([P, P, PACK], F32, "size_row")
         nc.scalar.activation(size_row[:], size_ps[:].rearrange("p t s -> p s t"), ACT.Copy)
 
-        keys_g = sb.tile([P, PACK, I], BF16, name="keys_g")
+        keys_g = tile([P, PACK, I], BF16, "keys_g")
         for j in range(PACK):
-            nc.vector.tensor_copy(keys_g[:, j, :], key_planes[j][:].indirect(offsets[:]))
-        keys_w = sb.tile([P, I * PACK], BF16, name="keys_w", align_bytes=64)
-        for eng, a, b in (("V", 0, KSPLIT), ("S", KSPLIT, I)):
-            if b > a:
-                cast(eng, keys_w[:, a * PACK:b * PACK].rearrange("p (c i t) -> p c t i", i=4, t=PACK),
-                     keys_g[:, :, a:b].rearrange("p t (c i) -> p c t i", i=4))
-        keys_q = quantise("keys", keys_w[:], I)
+            nc.vector.tensor_copy(keys_g[:, j, :], raw["k%d" % j][:].indirect(offsets[:]))
+        keys_w = tile([P, I * PACK], BF16, "keys_w")
+        k_codes = tile([P, I], U32, "keys_codes")
+        k_scales = tile([P, I], U8, "keys_scales")
+        keys_q = (k_codes, k_scales)
+        cast("S", keys_w[:].rearrange("p (i u t) -> p u i t", u=2, t=2)[:, 0], keys_g[:, 0:2, :].rearrange("p t i -> p i t"))
+        for a, b in [[0,256],[256,512]]:
+            cast("V", keys_w[:].rearrange("p (i u t) -> p u i t", u=2, t=2)[:, 1, a:b], keys_g[:, 2:4, a:b].rearrange("p t i -> p i t"))
+        for a, b in [[0,256],[256,512]]:
+            nc.vector.quantize_mx(out=k_codes[:, a:b].bitcast(FP8X4), scales=k_scales[:, a:b], in_=keys_w[:, a * PACK:b * PACK])
 
-        query_q = {}
-        w_q = {}
-        w_sb = {}
-        p_sb = {}
-        p_sum = {}
-        vals_q = {}
-        o_ps = {}
-        gate = {}
-        half_sum = sb.tile([P, PACK, X], F32, name="half_sum")
-        y = sb.tile([P, PACK, X], F32, name="y")
-        y_w = sb.tile([P, X * PACK], BF16, name="y_w", align_bytes=64)
+        st = {}
+        sums = tile([P, PACK, X], F32, "sums")
+        y = tile([P, PACK, X], F32, "y")
+        y_w = tile([P, X * PACK], BF16, "y_w")
+        w_codes = tile([P, Q], U32, "w_codes")
+        w_scales = tile([P, Q], U8, "w_scales")
 
-        ob_lo = sb.tile([P, PACK, 2 * P], F32, name="ob_lo")
+        def qi(h):
+            st["qw", h] = tile([P, Q // 2 * PACK], BF16, "query_w%d" % h)
+            cast(Q_ENG[h], st["qw", h][:].rearrange("p (c i t) -> p c t i", i=4, t=PACK),
+                 raw["q%d" % h][:].rearrange("p t (c i) -> p c t i", i=4))
 
-        def do_query(h):
-            query_w = sb.tile([P, Q // 2 * PACK], BF16, name="query_w%d" % h, align_bytes=64)
-            cast(Q_ENG[h], query_w[:].rearrange("p (c i t) -> p c t i", i=4, t=PACK),
-                 query_raw[h][:].rearrange("p t (c i) -> p c t i", i=4))
-            query_q[h] = quantise("query%d" % h, query_w[:], Q // 2)
+        def qq(h):
+            st["q", h] = quantise("query%d" % h, st["qw", h][:], Q // 2)
 
-        def do_exp(b):
-            a_ps = ps.tile([P, I], F32, name="a_ps%d" % b, tag="scores", bufs=2)
-            product(a_ps[:], query_q[b // 2], slice((b % 2) * P, (b % 2 + 1) * P), keys_q)
-            neg_max = sb.tile([P, 1], F32, name="neg_max%d" % b)
-            nc.vector.tensor_reduce(neg_max[:], a_ps[:], AXIS.X, ALU.max, negate=True)
-            p_sb[b] = sb.tile([P, I], F32, name="p_sb%d" % b)
-            p_sum[b] = sb.tile([P, 1], F32, name="p_sum%d" % b)
-            nc.scalar.activation(p_sb[b][:], a_ps[:], ACT.Exp, bias=neg_max[:], accum_out=p_sum[b][:])
+        def sc(b):
+            st["a", b] = ps.tile([P, I], F32, name="a_ps%d" % b, tag="big", bufs=4)
+            product(st["a", b][:], st["q", b // 2], slice((b % 2) * P, (b % 2 + 1) * P), keys_q)
 
-        def do_weights(b):
-            p_inv = sb.tile([P, 1], F32, name="p_inv%d" % b)
-            nc.vector.reciprocal(p_inv[:], p_sum[b][:])
-            w_sb = sb.tile([P, I], BF16, name="w_sb%d" % b)
-            nc.vector.scalar_tensor_tensor(w_sb[:], p_sb[b][:], p_inv[:], size_row[:].rearrange("p s t -> p (s t)"),
+        def mx(b):
+            st["m", b] = tile([P, 1], F32, "neg_max%d" % b)
+            nc.vector.tensor_reduce(st["m", b][:], st["a", b][:], AXIS.X, ALU.max, negate=True)
+
+        def ex(b):
+            st["p", b] = tile([P, I], F32, "p_sb%d" % b)
+            st["s", b] = tile([P, 1], F32, "p_sum%d" % b)
+            nc.scalar.activation(st["p", b][:], st["a", b][:], ACT.Exp, bias=st["m", b][:], accum_out=st["s", b][:])
+
+        def rc(b):
+            st["i", b] = tile([P, 1], F32, "p_inv%d" % b)
+            nc.vector.reciprocal(st["i", b][:], st["s", b][:])
+
+        def we(b):
+            w_sb = tile([P, I], BF16, "w_sb%d" % b)
+            nc.vector.scalar_tensor_tensor(w_sb[:], st["p", b][:], st["i", b][:], size_row[:].rearrange("p s t -> p (s t)"),
                                            ALU.mult, ALU.mult)
-            w_ps = ps.tile([P, 2, P], F32, name="w_ps%d" % b, tag="wturn", bufs=1)
+            w_ps = ps.tile([P, 2, P], F32, name="w_ps%d" % b, tag="wturn", bufs=2)
             for u in range(2):
                 nc.tensor.transpose(w_ps[:, u, :], w_sb[:].bitcast(F32)[:, u:I // 2:2], ident[:])
-            w_w = sb.tile([P, P * PACK], BF16, name="w_w%d" % b, align_bytes=64)
-            nc.scalar.copy(w_w[:].bitcast(F32).rearrange("p (q u) -> p q u", u=2), w_ps[:].rearrange("p u q -> p q u"))
-            w_q[b] = quantise("w%d" % b, w_w[:], P)
+            st["ww", b] = tile([P, P * PACK], BF16, "w_w%d" % b)
+            nc.scalar.copy(st["ww", b][:].bitcast(F32).rearrange("p (q u) -> p q u", u=2), w_ps[:].rearrange("p u q -> p q u"))
 
-        def do_vals(r):
-            vals_g = sb.tile([P, I], BF16, name="vals_g%d" % r)
-            nc.vector.tensor_copy(vals_g[:], val_planes[r][:].indirect(offsets[:]))
-            v_ps = ps.tile([P, 2, P], F32, name="v_ps%d" % r, tag="vturn", bufs=1)
+        def wq(b):
+            nc.vector.quantize_mx(out=w_codes[:, b * P:(b + 1) * P].bitcast(FP8X4), scales=w_scales[:, b * P:(b + 1) * P], in_=st["ww", b][:])
+
+        def vg(r):
+            vals_g = tile([P, I], BF16, "vals_g%d" % r)
+            nc.vector.tensor_copy(vals_g[:], raw["v%d" % r][:].indirect(offsets[:]))
+            v_ps = ps.tile([P, 2, P], F32, name="v_ps%d" % r, tag="misc" if r % 2 else "vturn", bufs=1)
             for u in range(2):
                 nc.tensor.transpose(v_ps[:, u, :], vals_g[:].bitcast(F32)[:, u:I // 2:2], ident[:])
-            v_w = sb.tile([P, P * PACK], BF16, name="v_w%d" % r, align_bytes=64)
-            nc.scalar.copy(v_w[:].bitcast(F32).rearrange("p (m u) -> p m u", u=2), v_ps[:].rearrange("p u m -> p m u"))
-            vals_q[r] = (quantise("v%d" % r, v_w[:], P), slice(0, P))
+            if r == 0:
+                st["vw01"] = tile([P, 2 * P * PACK], BF16, "v_w01")
+            st["vw", r] = st["vw01"][:, r * P * PACK:(r + 1) * P * PACK] if r < 2 else tile([P, P * PACK], BF16, "v_w%d" % r)
+            nc.scalar.copy(st["vw", r][:].bitcast(F32).rearrange("p (m u) -> p m u", u=2), v_ps[:].rearrange("p u m -> p m u"))
 
-        def do_pair(n):
-            pairs = sb.tile([P, T, 2], BF16, name="pairs%d" % n)
-            w = T // CASTN
-            for c in range(CASTN):
-                nc.scalar.activation(pairs[:, c * w:(c + 1) * w, :].rearrange("p (c i) r -> p c r i", i=4),
-                                     val_two[2 * n + c][:].rearrange("p r (c i) -> p c r i", i=4), ACT.Copy)
-            pairs_g = sb.tile([P, I], U32, name="pairs_g%d" % n)
-            nc.vector.tensor_copy(pairs_g[:], pairs[:].rearrange("p t r -> p (t r)").bitcast(U32).indirect(offsets[:]))
+        def vq(r):
+            if r < 2:
+                both = quantise("v01", st["vw01"][:], 2 * P)
+                st["v", 0] = (both, slice(0, P))
+                st["v", 1] = (both, slice(P, 2 * P))
+            else:
+                st["v", r] = (quantise("v%d" % r, st["vw", r][:], P), slice(0, P))
+
+        def pc(n):
+            if n % 2 == 0:
+                st["pairs", n // 2] = tile([P, T, 2], BF16, "pairs%d" % (n // 2))
+            w = T // 2
+            c = n % 2
+            nc.scalar.activation(st["pairs", n // 2][:, c * w:(c + 1) * w, :].rearrange("p (c i) r -> p c r i", i=4),
+                                 raw["p%d" % n][:].rearrange("p r (c i) -> p c r i", i=4), ACT.Copy)
+
+        def pg(n):
+            pairs_g = tile([P, I], U32, "pairs_g%d" % n)
+            nc.vector.tensor_copy(pairs_g[:], st["pairs", n][:].rearrange("p t r -> p (t r)").bitcast(U32).indirect(offsets[:]))
             v_ps = ps.tile([P, PACK, P], F32, name="vp_ps%d" % n, tag="vturn", bufs=1)
             for t in range(PACK):
                 nc.tensor.transpose(v_ps[:, t, :], pairs_g[:].bitcast(F32)[:, t:I:PACK], ident[:])
-            v_w = sb.tile([P, 2 * P * PACK], BF16, name="vp_w%d" % n, align_bytes=64)
-            nc.scalar.copy(v_w[:].rearrange("p (r m t) -> p r m t", r=2, t=PACK),
+            st["pw", n] = tile([P, 2 * P * PACK], BF16, "vp_w%d" % n)
+            nc.scalar.copy(st["pw", n][:].rearrange("p (r m t) -> p r m t", r=2, t=PACK),
                            v_ps[:].bitcast(BF16).rearrange("p t (m r) -> p r m t", r=2))
-            both = quantise("vp%d" % n, v_w[:], 2 * P)
+
+        def pq(n):
+            both = quantise("vp%d" % n, st["pw", n][:], 2 * P)
             for r in range(2):
-                vals_q[2 * n + r] = (both, slice(r * P, (r + 1) * P))
+                st["v", 2 * n + r] = (both, slice(r * P, (r + 1) * P))
 
-        def do_out(b):
-            o_ps = ps.tile([P, PACK, P], F32, name="o_ps%d" % b, tag="o", bufs=3)
-            for r in range(PACK):
-                product(o_ps[:, r, :], vals_q[r][0], vals_q[r][1], w_q[b])
-            if b < 2:
-                ob = ob_lo[:, :, b * P:(b + 1) * P]
-            else:
-                ob = sb.tile([P, PACK, P], F32, name="ob%d" % b)
+        def om(n):
+            b, r = n // 10, n % 10
+            if ("o", b) not in st:
+                st["o", b] = ps.tile([P, PACK, P], F32, name="o_ps%d" % b, tag="big", bufs=4)
+            lhs, lcols = st["v", r]
+            cols = slice(b * P, (b + 1) * P)
+            nc.tensor.matmul_mx(out=st["o", b][:, r, :], lhsT=lhs[0][:, lcols].bitcast(FP8X4), lhsT_scale=lhs[1][:, lcols],
+                                rhs=w_codes[:, cols].bitcast(FP8X4), rhs_scale=w_scales[:, cols], start=True, stop=True)
+
+        def ob(b):
             w = Q // OWNN
-            nc.vector.scalar_tensor_tensor(ob[:], o_ps[:], 0.5, own_sb[b * P // w][:, :, b * P % w:b * P % w + P], ALU.mult, ALU.mult)
-            if b >= 2:
-                nc.vector.tensor_reduce(half_sum[:, :, b * XT:(b + 1) * XT],
-                                        ob[:].rearrange("p r (x j) -> p r x j", j=HEADS), AXIS.X, ALU.add)
+            own_b = raw["o%d" % (b * P // w) if OWNN > 1 else "o"][:, :, b * P % w:b * P % w + P]
+            st["ob", b] = tile([P, Q], F32, "ob%d" % b)
+            if b in PE_R:
+                nc.vector.tensor_tensor(st["ob", b][:].rearrange("p (a r x c) -> p r x a c", a=4, r=PACK, c=2),
+                                        st["o", b][:].rearrange("p r (x a c) -> p r x a c", a=4, c=2),
+                                        own_b.rearrange("p r (x a c) -> p r x a c", a=4, c=2), ALU.mult)
+            else:
+                nc.vector.tensor_tensor(st["ob", b][:].rearrange("p (r q) -> p r q", r=PACK), st["o", b][:], own_b, ALU.mult)
 
-        def do_sum(n):
-            st_ps = ps.tile([P, P], F32, name="st_ps", tag="scores", bufs=2)
-            flat = ob_lo[:].rearrange("p r q -> p (r q)")
-            for j in range(HEADS):
-                nc.tensor.matmul(st_ps[:], lhsT=flat[:, j:PACK * 2 * P:HEADS], rhs=ident[:], start=(j == 0), stop=(j == HEADS - 1), is_transpose=True)
-            st_sb = sb.tile([P, P], F32, name="st_sb")
-            nc.scalar.copy(st_sb[:], st_ps[:])
-            gate[1] = ps.tile([P, P], F32, name="back_ps", tag="scores", bufs=2)
-            nc.tensor.transpose(gate[1][:], st_sb[:], ident[:])
+        def rd(b):
+            nc.vector.tensor_reduce(sums[:, :, b * XT:(b + 1) * XT],
+                                    st["ob", b][:].rearrange("p (r x j) -> p r x j", r=PACK, j=HEADS), AXIS.X, ALU.add)
 
-        def do_y(h):
-            cols = slice(h * X // 2, (h + 1) * X // 2)
-            src = half_sum[:, :, cols] if h else gate[1][:].rearrange("p (r x) -> p r x", r=PACK)
-            nc.vector.scalar_tensor_tensor(y[:, :, cols], gate[0][:, :, cols], 1.0, src, ALU.add, ALU.mult)
-            cast("V" if h else "S", y_w[:].rearrange("p (x r) -> p x r", r=PACK)[:, cols, :], y[:, :, cols].rearrange("p r x -> p x r"))
+        def su(b):
+            half = tile([P, Q // 2], F32, "half%d" % b)
+            nc.gpsimd.tensor_tensor(half[:], st["ob", b][:, :Q // 2], st["ob", b][:, Q // 2:], ALU.add)
+            quarter = tile([P, Q // 4], F32, "quarter%d" % b)
+            nc.gpsimd.tensor_tensor(quarter[:], half[:, :Q // 4], half[:, Q // 4:], ALU.add)
+            pairs = quarter[:].rearrange("p (r x c) -> p r x c", r=PACK, c=2)
+            nc.gpsimd.tensor_tensor(sums[:, :, b * XT:(b + 1) * XT], pairs[:, :, :, 0], pairs[:, :, :, 1], ALU.add)
 
-        def do_gate(n):
-            inp_w = sb.tile([P, X * PACK], BF16, name="inp_w", align_bytes=64)
-            nc.scalar.copy(inp_w[:].rearrange("p (c i t) -> p c t i", i=4, t=PACK),
-                           inp_raw[:].rearrange("p t (c i) -> p c t i", i=4))
-            inp_q = quantise("inp", inp_w[:], X)
-            wg_w = sb.tile([P, E * PACK], BF16, name="wg_w", align_bytes=64)
+        def gi(n):
+            st["iw"] = tile([P, X * PACK], BF16, "inp_w")
+            nc.scalar.copy(st["iw"][:].rearrange("p (c i t) -> p c t i", i=4, t=PACK),
+                           raw["i"][:].rearrange("p t (c i) -> p c t i", i=4))
+
+        def iq(n):
+            st["inp"] = quantise("inp", st["iw"][:], X)
+
+        def gw(c):
+            if c == 0:
+                st["gw"] = tile([P, E * PACK], BF16, "wg_w")
             w = P // WGN
-            for c in range(WGN):
-                cast(WG_ENG[c], wg_w[:].rearrange("p (r m t) -> p m t r", r=PACK, t=PACK)[:, c * w:(c + 1) * w],
-                     wg_raw[:].rearrange("p t (m r) -> p m t r", r=PACK)[:, c * w:(c + 1) * w])
-            wg_q = quantise("wg", wg_w[:], E)
-            g_ps = ps.tile([P, PACK, X], F32, name="g_ps", tag="g", bufs=1)
-            for r in range(PACK):
-                product(g_ps[:, r, :], wg_q, slice(r * P, (r + 1) * P), inp_q)
-            gate[0] = sb.tile([P, PACK, X], F32, name="g_tanh")
-            nc.scalar.activation(gate[0][:], g_ps[:], ACT.Tanh, scale=0.5)
+            cast(WG_ENG[c], st["gw"][:].rearrange("p (r m t) -> p m t r", r=PACK, t=PACK)[:, c * w:(c + 1) * w],
+                 raw["w"][:].rearrange("p t (m r) -> p m t r", r=PACK)[:, c * w:(c + 1) * w])
 
-        steps = {"q": do_query, "e": do_exp, "w": do_weights, "v": do_vals, "p": do_pair, "o": do_out, "g": do_gate, "s": do_sum, "y": do_y}
+        def gq(n):
+            wg_q = quantise("wg", st["gw"][:], E)
+            g_ps = ps.tile([P, PACK, X], F32, name="g_ps", tag="misc", bufs=1)
+            for r in range(PACK):
+                product(g_ps[:, r, :], wg_q, slice(r * P, (r + 1) * P), st["inp"])
+            g_tanh = tile([P, PACK, X], F32, "g_tanh")
+            nc.scalar.activation(g_tanh[:], g_ps[:], ACT.Tanh, scale=0.5)
+            st["gate"] = tile([P, PACK, X], F32, "gate")
+            nc.scalar.activation(st["gate"][:], g_tanh[:], ACT.Copy, scale=0.5, bias=0.5)
+
+        def ya(n):
+            cols = slice(n * X // 2, (n + 1) * X // 2)
+            nc.vector.tensor_tensor(y_w[:].rearrange("p (x r) -> p x r", r=PACK)[:, cols, :], sums[:, :, cols].rearrange("p r x -> p x r"),
+                                    st["gate"][:, :, cols].rearrange("p r x -> p x r"), ALU.mult)
+
+        def yb(n):
+            cols = slice(n * X // 2, (n + 1) * X // 2)
+            nc.vector.tensor_tensor(y[:, :, cols], sums[:, :, cols], st["gate"][:, :, cols], ALU.mult)
+
+        def yc(n):
+            nc.vector.tensor_tensor(y_w[:].rearrange("p (x r) -> p x r", r=PACK), sums[:].rearrange("p r x -> p x r"),
+                                    st["gate"][:].rearrange("p r x -> p x r"), ALU.mult)
+            nc.vector.tensor_tensor(y[:], sums[:], st["gate"][:], ALU.mult)
+
+        steps = {"qi": qi, "qq": qq, "sc": sc, "mx": mx, "ex": ex, "rc": rc, "we": we, "wq": wq, "vg": vg, "vq": vq, "pc": pc,
+                 "pg": pg, "pq": pq, "om": om, "ob": ob, "rd": rd, "su": su, "gi": gi, "iq": iq, "gw": gw, "gq": gq,
+                 "ya": ya, "yb": yb, "yc": yc}
         for name in ORDER:
-            steps[name[0]](int(name[1:]))
+            steps[name[:2]](int(name[2:]))
 
         nc.sync.dma_start(out_0.rearrange("(p r) x -> p r x", r=PACK), y[:])
         y_codes, y_scales = quantise("y", y_w[:], X)
-        nc.sync.dma_start(out_1[0].rearrange("p c r -> p (c r)").bitcast(I32), y_codes[:].bitcast(I32))
+        nc.scalar.dma_start(out_1[0].rearrange("p c r -> p (c r)").bitcast(I32), y_codes[:].bitcast(I32))
         for g in range(4):
-            eng = nc.scalar if g % 2 else nc.sync
+            eng = nc.scalar if g == 3 else nc.sync
             eng.dma_start(out_2[0, 4 * g:4 * g + 4, :].bitcast(I32), y_scales[32 * g:32 * g + 4, :].bitcast(I32))

@@ -23,7 +23,7 @@ HEADS = 8
 QT = Q // P
 XT = P // HEADS
 LOADS = ["k0","s","k1","k2","k3","q0","v0","q1","v1","w","v2","v3","i","o"]
-ORDER = ["qi0","qq0","sc0","sc1","vg0","qi1","mx0","ex0","mx1","ex1","qq1","sc2","sc3","gw0","gw1","gw2","gw3","vg1","rc0","rc1","we0","mx2","ex2","we1","mx3","ex3","vg2","vg3","rc2","wq0","we2","rc3","wq1","we3","vq0","vq2","vq3","om0","om1","om2","om3","om10","om11","om12","om13","gi0","iq0","gq0","wq2","wq3","om20","om21","om22","om23","om30","om31","om32","om33","ob0","su0","ob1","su1","ob2","ob3","rd2","rd3","ya0","yb0","ya1","yb1"]
+ORDER = ["qi0","qq0","sc0","sc1","vg0","qi1","mx0","ex0","mx1","ex1","qq1","sc2","sc3","gw0","gw1","gw2","gw3","vg1","rc0","rc1","we0","mx2","ex2","we1","mx3","ex3","vg2","vg3","rc2","wq0","we2","wq1","vq0","vq2","vq3","om0","om1","om2","om3","om10","om11","om12","om13","rc3","we3","gi0","iq0","ob0","su0","wq2","om20","om21","om22","om23","ob1","su1","wq3","om30","om31","om32","om33","gq0","ob2","rd2","ob3","yb0","ya0","rd3","yb1","ya1"]
 TAGS = {"vals_g0":"raw_q0","vals_g1":"raw_q1","vals_g2":"x2","w_sb0":"x2","vals_g3":"x3","w_sb1":"x3","v01_codes":"x4","p_sb2":"x4","wg_codes":"x5","v_w01":"x5"}
 KSPLIT = 512
 WGN = 4
@@ -31,6 +31,7 @@ OWNN = 1
 WG_ENG = "SSSS"
 Q_ENG = "SS"
 PE_R = [0,1]
+G_FULL = [0,1]
 CUTS = [[0,512]]
 
 
@@ -62,7 +63,6 @@ def tile_attend_ownlists_gate_pl_kernel(tc, query, keys, size, vals, own, inp, w
                 nc.gpsimd.tensor_scalar(out, in_, 1.0, 0.0, ALU.mult, ALU.add)
 
         offsets = sb.tile([P, I // 16], U16, name="offsets")
-        nc.sync.dma_start(offsets[:], offs)
         keys_v = keys.rearrange("(p j) t -> j p t", j=PACK)
         vals_v = vals.rearrange("(p j) t -> j p t", j=PACK)
         query_v = query.rearrange("(p j) q -> p j q", j=PACK)
@@ -89,6 +89,8 @@ def tile_attend_ownlists_gate_pl_kernel(tc, query, keys, size, vals, own, inp, w
                 shape, src = [P, PACK, E], wg_v
             raw[name] = tile(shape, F32, "raw_" + name)
             nc.sync.dma_start(raw[name][:], src)
+            if name == "k0":
+                nc.sync.dma_start(offsets[:], offs)
 
         ident = sb.tile([P, P], F32, name="ident")
         make_identity(nc, ident[:])
@@ -112,6 +114,8 @@ def tile_attend_ownlists_gate_pl_kernel(tc, query, keys, size, vals, own, inp, w
         for a, b in [[0,256],[256,512]]:
             nc.vector.quantize_mx(out=k_codes[:, a:b].bitcast(FP8X4), scales=k_scales[:, a:b], in_=keys_w[:, a * PACK:b * PACK])
 
+        minus_one = tile([P, 1], F32, "minus_one")
+        nc.gpsimd.memset(minus_one[:], -1.0)
         st = {}
         sums = tile([P, PACK, X], F32, "sums")
         y = tile([P, PACK, X], F32, "y")
@@ -142,7 +146,7 @@ def tile_attend_ownlists_gate_pl_kernel(tc, query, keys, size, vals, own, inp, w
 
         def rc(b):
             st["i", b] = tile([P, 1], F32, "p_inv%d" % b)
-            nc.vector.reciprocal(st["i", b][:], st["s", b][:])
+            nc.gpsimd.tensor_tensor(st["i", b][:], st["s", b][:], minus_one[:], ALU.pow)
 
         def we(b):
             w_sb = tile([P, I], BF16, "w_sb%d" % b)
@@ -212,24 +216,27 @@ def tile_attend_ownlists_gate_pl_kernel(tc, query, keys, size, vals, own, inp, w
             w = Q // OWNN
             own_b = raw["o%d" % (b * P // w) if OWNN > 1 else "o"][:, :, b * P % w:b * P % w + P]
             st["ob", b] = tile([P, Q], F32, "ob%d" % b)
-            if b in PE_R:
-                nc.vector.tensor_tensor(st["ob", b][:].rearrange("p (a r x c) -> p r x a c", a=4, r=PACK, c=2),
-                                        st["o", b][:].rearrange("p r (x a c) -> p r x a c", a=4, c=2),
-                                        own_b.rearrange("p r (x a c) -> p r x a c", a=4, c=2), ALU.mult)
-            else:
-                nc.vector.tensor_tensor(st["ob", b][:].rearrange("p (r q) -> p r q", r=PACK), st["o", b][:], own_b, ALU.mult)
+            nc.vector.tensor_tensor(st["ob", b][:].rearrange("p (r q) -> p r q", r=PACK), st["o", b][:], own_b, ALU.mult)
 
         def rd(b):
             nc.vector.tensor_reduce(sums[:, :, b * XT:(b + 1) * XT],
                                     st["ob", b][:].rearrange("p (r x j) -> p r x j", r=PACK, j=HEADS), AXIS.X, ALU.add)
 
         def su(b):
-            half = tile([P, Q // 2], F32, "half%d" % b)
-            nc.gpsimd.tensor_tensor(half[:], st["ob", b][:, :Q // 2], st["ob", b][:, Q // 2:], ALU.add)
-            quarter = tile([P, Q // 4], F32, "quarter%d" % b)
-            nc.gpsimd.tensor_tensor(quarter[:], half[:, :Q // 4], half[:, Q // 4:], ALU.add)
-            pairs = quarter[:].rearrange("p (r x c) -> p r x c", r=PACK, c=2)
-            nc.gpsimd.tensor_tensor(sums[:, :, b * XT:(b + 1) * XT], pairs[:, :, :, 0], pairs[:, :, :, 1], ALU.add)
+            src = st["ob", b]
+            for w in (4, 2):
+                dst = tile([P, PACK * XT * w], F32, "part%d_%d" % (b, w))
+                both = src[:].rearrange("p (m h c) -> p m h c", h=2, c=w)
+                nc.gpsimd.tensor_tensor(dst[:].rearrange("p (m c) -> p m c", c=w), both[:, :, 0, :], both[:, :, 1, :], ALU.add)
+                src = dst
+            pairs = src[:].rearrange("p (r x c) -> p r x c", r=PACK, c=2)
+            if b in G_FULL:
+                nc.gpsimd.tensor_tensor(sums[:, :, b * XT:(b + 1) * XT], pairs[:, :, :, 0], pairs[:, :, :, 1], ALU.add)
+            else:
+                st["pairs", b] = pairs
+
+        def sv(b):
+            nc.vector.tensor_reduce(sums[:, :, b * XT:(b + 1) * XT], st["pairs", b], AXIS.X, ALU.add)
 
         def gi(n):
             st["iw"] = tile([P, X * PACK], BF16, "inp_w")
@@ -258,8 +265,7 @@ def tile_attend_ownlists_gate_pl_kernel(tc, query, keys, size, vals, own, inp, w
 
         def ya(n):
             cols = slice(n * X // 2, (n + 1) * X // 2)
-            nc.vector.tensor_tensor(y_w[:].rearrange("p (x r) -> p x r", r=PACK)[:, cols, :], sums[:, :, cols].rearrange("p r x -> p x r"),
-                                    st["gate"][:, :, cols].rearrange("p r x -> p x r"), ALU.mult)
+            cast("V", y_w[:].rearrange("p (x r) -> p x r", r=PACK)[:, cols, :], y[:, :, cols].rearrange("p r x -> p x r"))
 
         def yb(n):
             cols = slice(n * X // 2, (n + 1) * X // 2)
@@ -272,13 +278,13 @@ def tile_attend_ownlists_gate_pl_kernel(tc, query, keys, size, vals, own, inp, w
 
         steps = {"qi": qi, "qq": qq, "sc": sc, "mx": mx, "ex": ex, "rc": rc, "we": we, "wq": wq, "vg": vg, "vq": vq, "pc": pc,
                  "pg": pg, "pq": pq, "om": om, "ob": ob, "rd": rd, "su": su, "gi": gi, "iq": iq, "gw": gw, "gq": gq,
-                 "ya": ya, "yb": yb, "yc": yc}
+                 "sv": sv, "ya": ya, "yb": yb, "yc": yc}
         for name in ORDER:
             steps[name[:2]](int(name[2:]))
 
-        nc.sync.dma_start(out_0.rearrange("(p r) x -> p r x", r=PACK), y[:])
+        nc.scalar.dma_start(out_0.rearrange("(p r) x -> p r x", r=PACK), y[:])
         y_codes, y_scales = quantise("y", y_w[:], X)
-        nc.scalar.dma_start(out_1[0].rearrange("p c r -> p (c r)").bitcast(I32), y_codes[:].bitcast(I32))
+        nc.sync.dma_start(out_1[0].rearrange("p c r -> p (c r)").bitcast(I32), y_codes[:].bitcast(I32))
         for g in range(4):
-            eng = nc.scalar if g == 3 else nc.sync
+            eng = nc.scalar if g % 2 else nc.sync
             eng.dma_start(out_2[0, 4 * g:4 * g + 4, :].bitcast(I32), y_scales[32 * g:32 * g + 4, :].bitcast(I32))

@@ -20,19 +20,11 @@ AXIS = mybir.AxisListType
 P = 128
 PACK = 4
 HEADS = 8
-QT = Q // P
-XT = P // HEADS
-LOADS = ["k0","s","k1","k2","k3","q0","v0","q1","v1","w","v2","v3","i","o"]
-ORDER = ["qi0","qq0","sc0","sc1","vg0","qi1","mx0","ex0","mx1","ex1","qq1","sc2","sc3","gw0","gw1","gw2","gw3","vg1","rc0","rc1","we0","mx2","ex2","we1","mx3","ex3","vg2","vg3","rc2","wq0","we2","wq1","vq0","vq2","vq3","om0","om1","om2","om3","om10","om11","om12","om13","rc3","we3","gi0","iq0","ob0","su0","wq2","om20","om21","om22","om23","ob1","su1","wq3","om30","om31","om32","om33","gq0","ob2","rd2","ob3","yb0","ya0","rd3","yb1","ya1"]
-TAGS = {"vals_g0":"raw_q0","vals_g1":"raw_q1","vals_g2":"x2","w_sb0":"x2","vals_g3":"x3","w_sb1":"x3","v01_codes":"x4","p_sb2":"x4","wg_codes":"x5","v_w01":"x5"}
-KSPLIT = 512
-WGN = 4
-OWNN = 1
-WG_ENG = "SSSS"
-Q_ENG = "SS"
-PE_R = [0,1]
-G_FULL = [0,1]
-CUTS = [[0,512]]
+LINE = 4
+TILES = Q // P
+PLACES = P // HEADS
+WG_PIECES = 4
+LAST = TILES - 1
 
 
 def tile_attend_ownlists_gate_pl_kernel(tc, query, keys, size, vals, own, inp, wg, offs, out_0, out_1, out_2):
@@ -41,250 +33,213 @@ def tile_attend_ownlists_gate_pl_kernel(tc, query, keys, size, vals, own, inp, w
         sb = ctx.enter_context(tc.tile_pool(name="sb", bufs=1))
         ps = ctx.enter_context(tc.psum_pool(name="ps", bufs=1))
 
-        def tile(shape, dtype, name):
-            return sb.tile(shape, dtype, name=name, tag=TAGS.get(name, name), align_bytes=64)
+        reuses = {
+            "vals_g0": "query_raw0",
+            "vals_g1": "query_raw1",
+            "vals_g2": "w0",
+            "vals_g3": "w1",
+            "vals01_codes": "w2",
+            "wg_codes": "vals01_words",
+            "inp_codes": "w3_words",
+        }
 
-        def quantise(name, grouped, words):
-            codes = tile([P, words], U32, name + "_codes")
-            scales = tile([P, words], U8, name + "_scales")
-            nc.vector.quantize_mx(out=codes[:].bitcast(FP8X4), scales=scales[:], in_=grouped)
+        def tile(shape, dtype, name):
+            return sb.tile(shape, dtype, name=name, tag=reuses.get(name, name), align_bytes=64)
+
+        def load(shape, name, source):
+            raw = tile(shape, F32, name)
+            nc.sync.dma_start(raw[:], source)
+            return raw
+
+        def quantise(name, words, columns):
+            codes = tile([P, columns], U32, name + "_codes")
+            scales = tile([P, columns], U8, name + "_scales")
+            nc.vector.quantize_mx(out=codes[:].bitcast(FP8X4), scales=scales[:], in_=words)
             return codes, scales
 
-        def product(out, lhs, lcols, rhs):
-            nc.tensor.matmul_mx(out=out, lhsT=lhs[0][:, lcols].bitcast(FP8X4), lhsT_scale=lhs[1][:, lcols],
+        def product(out, lhs, lhs_cols, rhs):
+            nc.tensor.matmul_mx(out=out, lhsT=lhs[0][:, lhs_cols].bitcast(FP8X4), lhsT_scale=lhs[1][:, lhs_cols],
                                 rhs=rhs[0][:].bitcast(FP8X4), rhs_scale=rhs[1][:], start=True, stop=True)
 
-        def cast(eng, out, in_):
-            if eng == "S":
-                nc.scalar.copy(out, in_)
-            elif eng == "V":
-                nc.vector.tensor_copy(out, in_)
-            else:
-                nc.gpsimd.tensor_scalar(out, in_, 1.0, 0.0, ALU.mult, ALU.add)
+        def interleave(name, planes, columns):
+            words = tile([P, columns * PACK], BF16, name)
+            nc.scalar.copy(words[:].rearrange("p (c i t) -> p c t i", i=LINE, t=PACK),
+                           planes[:].rearrange("p t (c i) -> p c t i", i=LINE))
+            return words
 
-        offsets = sb.tile([P, I // 16], U16, name="offsets")
+        def turn(words, rows, bank):
+            for u in range(2):
+                nc.tensor.transpose(bank[:, u, :], rows[:].bitcast(F32)[:, u:I // 2:2], ident[:])
+            nc.scalar.copy(words.bitcast(F32).rearrange("p (c u) -> p c u", u=2), bank[:].rearrange("p u c -> p c u"))
+
         keys_v = keys.rearrange("(p j) t -> j p t", j=PACK)
         vals_v = vals.rearrange("(p j) t -> j p t", j=PACK)
         query_v = query.rearrange("(p j) q -> p j q", j=PACK)
-        own_v = own.rearrange("(p j) q -> p j q", j=PACK)
-        wg_v = wg.rearrange("(p j) e -> p j e", j=PACK)
-        raw = {}
-        for name in LOADS:
-            n = int(name[1:] or "0")
-            if name[0] == "k":
-                shape, src = [P, T], keys_v[n]
-            elif name[0] == "s":
-                shape, src = [P, PACK], size.rearrange("o (s t) -> s (o t)", t=PACK)
-            elif name[0] == "q":
-                shape, src = [P, PACK, Q // 2], query_v[:, :, n * (Q // 2):(n + 1) * (Q // 2)]
-            elif name[0] == "v":
-                shape, src = [P, T], vals_v[n]
-            elif name[0] == "p":
-                shape, src = [P, 2, T // 2], vals.rearrange("(p j) t -> p j t", j=PACK)[:, 2 * (n // 2):2 * (n // 2) + 2, (n % 2) * (T // 2):(n % 2 + 1) * (T // 2)]
-            elif name[0] == "o":
-                shape, src = [P, PACK, Q // OWNN], own_v[:, :, n * (Q // OWNN):(n + 1) * (Q // OWNN)]
-            elif name[0] == "i":
-                shape, src = [P, PACK, X], inp.rearrange("(p j) x -> p j x", j=PACK)
-            else:
-                shape, src = [P, PACK, E], wg_v
-            raw[name] = tile(shape, F32, "raw_" + name)
-            nc.sync.dma_start(raw[name][:], src)
-            if name == "k0":
-                nc.sync.dma_start(offsets[:], offs)
+        offsets = sb.tile([P, I // 16], U16, name="offsets")
+        key_planes = [load([P, T], "key_plane0", keys_v[0])]
+        nc.sync.dma_start(offsets[:], offs)
+        size_cols = load([P, PACK], "size_cols", size.rearrange("o (s t) -> s (o t)", t=PACK))
+        key_planes.extend(load([P, T], "key_plane%d" % j, keys_v[j]) for j in range(1, PACK))
+        query_raw, val_planes = [], []
+        for h in range(2):
+            query_raw.append(load([P, PACK, Q // 2], "query_raw%d" % h, query_v[:, :, h * (Q // 2):(h + 1) * (Q // 2)]))
+            val_planes.append(load([P, T], "val_plane%d" % h, vals_v[h]))
+        wg_raw = load([P, PACK, E], "wg_raw", wg.rearrange("(p j) e -> p j e", j=PACK))
+        val_planes.extend(load([P, T], "val_plane%d" % j, vals_v[j]) for j in range(2, PACK))
+        inp_raw = load([P, PACK, X], "inp_raw", inp.rearrange("(p j) x -> p j x", j=PACK))
+        own_sb = load([P, PACK, Q], "own_sb", own.rearrange("(p j) q -> p j q", j=PACK))
 
         ident = sb.tile([P, P], F32, name="ident")
         make_identity(nc, ident[:])
 
         size_ps = ps.tile([P, PACK, P], F32, name="size_ps", tag="misc", bufs=1)
         for t in range(PACK):
-            nc.tensor.transpose(size_ps[:, t, :], raw["s"][:, t:t + 1].to_broadcast([P, P]), ident[:])
+            nc.tensor.transpose(size_ps[:, t, :], size_cols[:, t:t + 1].to_broadcast([P, P]), ident[:])
         size_row = tile([P, P, PACK], F32, "size_row")
         nc.scalar.activation(size_row[:], size_ps[:].rearrange("p t s -> p s t"), ACT.Copy)
 
         keys_g = tile([P, PACK, I], BF16, "keys_g")
         for j in range(PACK):
-            nc.vector.tensor_copy(keys_g[:, j, :], raw["k%d" % j][:].indirect(offsets[:]))
-        keys_w = tile([P, I * PACK], BF16, "keys_w")
-        k_codes = tile([P, I], U32, "keys_codes")
-        k_scales = tile([P, I], U8, "keys_scales")
-        keys_q = (k_codes, k_scales)
-        cast("S", keys_w[:].rearrange("p (i u t) -> p u i t", u=2, t=2)[:, 0], keys_g[:, 0:2, :].rearrange("p t i -> p i t"))
-        for a, b in [[0,256],[256,512]]:
-            cast("V", keys_w[:].rearrange("p (i u t) -> p u i t", u=2, t=2)[:, 1, a:b], keys_g[:, 2:4, a:b].rearrange("p t i -> p i t"))
-        for a, b in [[0,256],[256,512]]:
-            nc.vector.quantize_mx(out=k_codes[:, a:b].bitcast(FP8X4), scales=k_scales[:, a:b], in_=keys_w[:, a * PACK:b * PACK])
+            nc.vector.tensor_copy(keys_g[:, j, :], key_planes[j][:].indirect(offsets[:]))
+        keys_words = tile([P, I * PACK], BF16, "keys_words")
+        keys_q = (tile([P, I], U32, "keys_codes"), tile([P, I], U8, "keys_scales"))
+        by_pair = keys_words[:].rearrange("p (i u t) -> p u i t", u=2, t=2)
+        nc.scalar.copy(by_pair[:, 0], keys_g[:, 0:2, :].rearrange("p t i -> p i t"))
+        halves = [slice(0, I // 2), slice(I // 2, I)]
+        for half in halves:
+            nc.vector.tensor_copy(by_pair[:, 1, half], keys_g[:, 2:4, half].rearrange("p t i -> p i t"))
+        for half in halves:
+            nc.vector.quantize_mx(out=keys_q[0][:, half].bitcast(FP8X4), scales=keys_q[1][:, half],
+                                  in_=keys_words[:, half.start * PACK:half.stop * PACK])
 
-        minus_one = tile([P, 1], F32, "minus_one")
-        nc.gpsimd.memset(minus_one[:], -1.0)
-        st = {}
         sums = tile([P, PACK, X], F32, "sums")
         y = tile([P, PACK, X], F32, "y")
-        y_w = tile([P, X * PACK], BF16, "y_w")
-        w_codes = tile([P, Q], U32, "w_codes")
-        w_scales = tile([P, Q], U8, "w_scales")
+        y_words = tile([P, X * PACK], BF16, "y_words")
+        scores, p_exp, p_sum, p_inv, w_words, w_q, val_words, o_ps, masked, halved = ({} for n in range(10))
 
-        def qi(h):
-            st["qw", h] = tile([P, Q // 2 * PACK], BF16, "query_w%d" % h)
-            cast(Q_ENG[h], st["qw", h][:].rearrange("p (c i t) -> p c t i", i=4, t=PACK),
-                 raw["q%d" % h][:].rearrange("p t (c i) -> p c t i", i=4))
+        def score_pair(h, query_words):
+            query_q = quantise("query%d" % h, query_words[:], Q // 2)
+            for b in (2 * h, 2 * h + 1):
+                scores[b] = ps.tile([P, I], F32, name="scores%d" % b, tag="big", bufs=4)
+                product(scores[b][:], query_q, slice((b % 2) * P, (b % 2 + 1) * P), keys_q)
 
-        def qq(h):
-            st["q", h] = quantise("query%d" % h, st["qw", h][:], Q // 2)
+        def exponentials(b):
+            neg_max = tile([P, 1], F32, "neg_max%d" % b)
+            nc.vector.tensor_reduce(neg_max[:], scores[b][:], AXIS.X, ALU.max, negate=True)
+            p_exp[b] = tile([P, I], F32, "p_exp%d" % b)
+            p_sum[b] = tile([P, 1], F32, "p_sum%d" % b)
+            nc.scalar.activation(p_exp[b][:], scores[b][:], ACT.Exp, bias=neg_max[:], accum_out=p_sum[b][:])
 
-        def sc(b):
-            st["a", b] = ps.tile([P, I], F32, name="a_ps%d" % b, tag="big", bufs=4)
-            product(st["a", b][:], st["q", b // 2], slice((b % 2) * P, (b % 2 + 1) * P), keys_q)
+        def invert_sum(b):
+            p_inv[b] = tile([P, 1], F32, "p_inv%d" % b)
+            nc.vector.reciprocal(p_inv[b][:], p_sum[b][:])
 
-        def mx(b):
-            st["m", b] = tile([P, 1], F32, "neg_max%d" % b)
-            nc.vector.tensor_reduce(st["m", b][:], st["a", b][:], AXIS.X, ALU.max, negate=True)
-
-        def ex(b):
-            st["p", b] = tile([P, I], F32, "p_sb%d" % b)
-            st["s", b] = tile([P, 1], F32, "p_sum%d" % b)
-            nc.scalar.activation(st["p", b][:], st["a", b][:], ACT.Exp, bias=st["m", b][:], accum_out=st["s", b][:])
-
-        def rc(b):
-            st["i", b] = tile([P, 1], F32, "p_inv%d" % b)
-            nc.gpsimd.tensor_tensor(st["i", b][:], st["s", b][:], minus_one[:], ALU.pow)
-
-        def we(b):
-            w_sb = tile([P, I], BF16, "w_sb%d" % b)
-            nc.vector.scalar_tensor_tensor(w_sb[:], st["p", b][:], st["i", b][:], size_row[:].rearrange("p s t -> p (s t)"),
+        def weights(b):
+            w = tile([P, I], BF16, "w%d" % b)
+            nc.vector.scalar_tensor_tensor(w[:], p_exp[b][:], p_inv[b][:], size_row[:].rearrange("p s t -> p (s t)"),
                                            ALU.mult, ALU.mult)
-            w_ps = ps.tile([P, 2, P], F32, name="w_ps%d" % b, tag="wturn", bufs=2)
-            for u in range(2):
-                nc.tensor.transpose(w_ps[:, u, :], w_sb[:].bitcast(F32)[:, u:I // 2:2], ident[:])
-            st["ww", b] = tile([P, P * PACK], BF16, "w_w%d" % b)
-            nc.scalar.copy(st["ww", b][:].bitcast(F32).rearrange("p (q u) -> p q u", u=2), w_ps[:].rearrange("p u q -> p q u"))
+            bank = ps.tile([P, 2, P], F32, name="w_ps%d" % b, tag="w_turn", bufs=2)
+            w_words[b] = tile([P, P * PACK], BF16, "w%d_words" % b)
+            turn(w_words[b][:], w, bank)
 
-        def wq(b):
-            nc.vector.quantize_mx(out=w_codes[:, b * P:(b + 1) * P].bitcast(FP8X4), scales=w_scales[:, b * P:(b + 1) * P], in_=st["ww", b][:])
-
-        def vg(r):
+        def gather_values(r, words):
             vals_g = tile([P, I], BF16, "vals_g%d" % r)
-            nc.vector.tensor_copy(vals_g[:], raw["v%d" % r][:].indirect(offsets[:]))
-            v_ps = ps.tile([P, 2, P], F32, name="v_ps%d" % r, tag="misc" if r % 2 else "vturn", bufs=1)
-            for u in range(2):
-                nc.tensor.transpose(v_ps[:, u, :], vals_g[:].bitcast(F32)[:, u:I // 2:2], ident[:])
-            if r == 0:
-                st["vw01"] = tile([P, 2 * P * PACK], BF16, "v_w01")
-            st["vw", r] = st["vw01"][:, r * P * PACK:(r + 1) * P * PACK] if r < 2 else tile([P, P * PACK], BF16, "v_w%d" % r)
-            nc.scalar.copy(st["vw", r][:].bitcast(F32).rearrange("p (m u) -> p m u", u=2), v_ps[:].rearrange("p u m -> p m u"))
+            nc.vector.tensor_copy(vals_g[:], val_planes[r][:].indirect(offsets[:]))
+            bank = ps.tile([P, 2, P], F32, name="v_ps%d" % r, tag="misc" if r % 2 else "v_turn", bufs=1)
+            turn(words, vals_g, bank)
 
-        def vq(r):
-            if r < 2:
-                both = quantise("v01", st["vw01"][:], 2 * P)
-                st["v", 0] = (both, slice(0, P))
-                st["v", 1] = (both, slice(P, 2 * P))
-            else:
-                st["v", r] = (quantise("v%d" % r, st["vw", r][:], P), slice(0, P))
-
-        def pc(n):
-            if n % 2 == 0:
-                st["pairs", n // 2] = tile([P, T, 2], BF16, "pairs%d" % (n // 2))
-            w = T // 2
-            c = n % 2
-            nc.scalar.activation(st["pairs", n // 2][:, c * w:(c + 1) * w, :].rearrange("p (c i) r -> p c r i", i=4),
-                                 raw["p%d" % n][:].rearrange("p r (c i) -> p c r i", i=4), ACT.Copy)
-
-        def pg(n):
-            pairs_g = tile([P, I], U32, "pairs_g%d" % n)
-            nc.vector.tensor_copy(pairs_g[:], st["pairs", n][:].rearrange("p t r -> p (t r)").bitcast(U32).indirect(offsets[:]))
-            v_ps = ps.tile([P, PACK, P], F32, name="vp_ps%d" % n, tag="vturn", bufs=1)
-            for t in range(PACK):
-                nc.tensor.transpose(v_ps[:, t, :], pairs_g[:].bitcast(F32)[:, t:I:PACK], ident[:])
-            st["pw", n] = tile([P, 2 * P * PACK], BF16, "vp_w%d" % n)
-            nc.scalar.copy(st["pw", n][:].rearrange("p (r m t) -> p r m t", r=2, t=PACK),
-                           v_ps[:].bitcast(BF16).rearrange("p t (m r) -> p r m t", r=2))
-
-        def pq(n):
-            both = quantise("vp%d" % n, st["pw", n][:], 2 * P)
-            for r in range(2):
-                st["v", 2 * n + r] = (both, slice(r * P, (r + 1) * P))
-
-        def om(n):
-            b, r = n // 10, n % 10
-            if ("o", b) not in st:
-                st["o", b] = ps.tile([P, PACK, P], F32, name="o_ps%d" % b, tag="big", bufs=4)
-            lhs, lcols = st["v", r]
-            cols = slice(b * P, (b + 1) * P)
-            nc.tensor.matmul_mx(out=st["o", b][:, r, :], lhsT=lhs[0][:, lcols].bitcast(FP8X4), lhsT_scale=lhs[1][:, lcols],
-                                rhs=w_codes[:, cols].bitcast(FP8X4), rhs_scale=w_scales[:, cols], start=True, stop=True)
-
-        def ob(b):
-            w = Q // OWNN
-            own_b = raw["o%d" % (b * P // w) if OWNN > 1 else "o"][:, :, b * P % w:b * P % w + P]
-            st["ob", b] = tile([P, Q], F32, "ob%d" % b)
-            nc.vector.tensor_tensor(st["ob", b][:].rearrange("p (r q) -> p r q", r=PACK), st["o", b][:], own_b, ALU.mult)
-
-        def rd(b):
-            nc.vector.tensor_reduce(sums[:, :, b * XT:(b + 1) * XT],
-                                    st["ob", b][:].rearrange("p (r x j) -> p r x j", r=PACK, j=HEADS), AXIS.X, ALU.add)
-
-        def su(b):
-            src = st["ob", b]
-            for w in (4, 2):
-                dst = tile([P, PACK * XT * w], F32, "part%d_%d" % (b, w))
-                both = src[:].rearrange("p (m h c) -> p m h c", h=2, c=w)
-                nc.gpsimd.tensor_tensor(dst[:].rearrange("p (m c) -> p m c", c=w), both[:, :, 0, :], both[:, :, 1, :], ALU.add)
-                src = dst
-            pairs = src[:].rearrange("p (r x c) -> p r x c", r=PACK, c=2)
-            if b in G_FULL:
-                nc.gpsimd.tensor_tensor(sums[:, :, b * XT:(b + 1) * XT], pairs[:, :, :, 0], pairs[:, :, :, 1], ALU.add)
-            else:
-                st["pairs", b] = pairs
-
-        def sv(b):
-            nc.vector.tensor_reduce(sums[:, :, b * XT:(b + 1) * XT], st["pairs", b], AXIS.X, ALU.add)
-
-        def gi(n):
-            st["iw"] = tile([P, X * PACK], BF16, "inp_w")
-            nc.scalar.copy(st["iw"][:].rearrange("p (c i t) -> p c t i", i=4, t=PACK),
-                           raw["i"][:].rearrange("p t (c i) -> p c t i", i=4))
-
-        def iq(n):
-            st["inp"] = quantise("inp", st["iw"][:], X)
-
-        def gw(c):
-            if c == 0:
-                st["gw"] = tile([P, E * PACK], BF16, "wg_w")
-            w = P // WGN
-            cast(WG_ENG[c], st["gw"][:].rearrange("p (r m t) -> p m t r", r=PACK, t=PACK)[:, c * w:(c + 1) * w],
-                 raw["w"][:].rearrange("p t (m r) -> p m t r", r=PACK)[:, c * w:(c + 1) * w])
-
-        def gq(n):
-            wg_q = quantise("wg", st["gw"][:], E)
-            g_ps = ps.tile([P, PACK, X], F32, name="g_ps", tag="misc", bufs=1)
+        def second_product(b):
+            o_ps[b] = ps.tile([P, PACK, P], F32, name="o_ps%d" % b, tag="big", bufs=4)
             for r in range(PACK):
-                product(g_ps[:, r, :], wg_q, slice(r * P, (r + 1) * P), st["inp"])
-            g_tanh = tile([P, PACK, X], F32, "g_tanh")
-            nc.scalar.activation(g_tanh[:], g_ps[:], ACT.Tanh, scale=0.5)
-            st["gate"] = tile([P, PACK, X], F32, "gate")
-            nc.scalar.activation(st["gate"][:], g_tanh[:], ACT.Copy, scale=0.5, bias=0.5)
+                product(o_ps[b][:, r, :], vals_q[r][0], vals_q[r][1], w_q[b])
 
-        def ya(n):
-            cols = slice(n * X // 2, (n + 1) * X // 2)
-            cast("V", y_w[:].rearrange("p (x r) -> p x r", r=PACK)[:, cols, :], y[:, :, cols].rearrange("p r x -> p x r"))
+        def times_own(b):
+            own_b = own_sb[:, :, b * P:(b + 1) * P]
+            masked[b] = tile([P, Q], F32, "masked%d" % b)
+            if b == LAST:
+                nc.vector.tensor_tensor(masked[b][:].rearrange("p (r q) -> p r q", r=PACK), o_ps[b][:], own_b, ALU.mult)
+            else:
+                nc.vector.tensor_tensor(masked[b][:].rearrange("p (h r x c) -> p r x h c", h=2, r=PACK, c=HEADS // 2),
+                                        o_ps[b][:].rearrange("p r (x h c) -> p r x h c", h=2, c=HEADS // 2),
+                                        own_b.rearrange("p r (x h c) -> p r x h c", h=2, c=HEADS // 2), ALU.mult)
 
-        def yb(n):
-            cols = slice(n * X // 2, (n + 1) * X // 2)
-            nc.vector.tensor_tensor(y[:, :, cols], sums[:, :, cols], st["gate"][:, :, cols], ALU.mult)
+        def add_halves(b):
+            halved[b] = tile([P, Q // 2], F32, "halved%d" % b)
+            nc.gpsimd.tensor_tensor(halved[b][:], masked[b][:, :Q // 2], masked[b][:, Q // 2:], ALU.add)
 
-        def yc(n):
-            nc.vector.tensor_tensor(y_w[:].rearrange("p (x r) -> p x r", r=PACK), sums[:].rearrange("p r x -> p x r"),
-                                    st["gate"][:].rearrange("p r x -> p x r"), ALU.mult)
-            nc.vector.tensor_tensor(y[:], sums[:], st["gate"][:], ALU.mult)
+        def sum_places(b):
+            terms = masked[b] if b == LAST else halved[b]
+            nc.vector.tensor_reduce(sums[:, :, b * PLACES:(b + 1) * PLACES],
+                                    terms[:].rearrange("p (r x c) -> p r x c", r=PACK, x=PLACES), AXIS.X, ALU.add)
 
-        steps = {"qi": qi, "qq": qq, "sc": sc, "mx": mx, "ex": ex, "rc": rc, "we": we, "wq": wq, "vg": vg, "vq": vq, "pc": pc,
-                 "pg": pg, "pq": pq, "om": om, "ob": ob, "rd": rd, "su": su, "gi": gi, "iq": iq, "gw": gw, "gq": gq,
-                 "sv": sv, "ya": ya, "yb": yb, "yc": yc}
-        for name in ORDER:
-            steps[name[:2]](int(name[2:]))
+        vals01_words = tile([P, 2 * P * PACK], BF16, "vals01_words")
+        score_pair(0, interleave("query_words0", query_raw[0], Q // 2))
+        gather_values(0, vals01_words[:, :P * PACK])
+        query_words1 = interleave("query_words1", query_raw[1], Q // 2)
+        for b in (0, 1):
+            exponentials(b)
+        score_pair(1, query_words1)
+        gather_values(1, vals01_words[:, P * PACK:])
+        for b in (0, 1):
+            invert_sum(b)
 
+        wg_words = tile([P, E * PACK], BF16, "wg_words")
+        piece = P // WG_PIECES
+        for c in range(WG_PIECES):
+            nc.scalar.copy(wg_words[:].rearrange("p (r m t) -> p m t r", r=PACK, t=PACK)[:, c * piece:(c + 1) * piece],
+                           wg_raw[:].rearrange("p t (m r) -> p m t r", r=PACK)[:, c * piece:(c + 1) * piece])
+
+        for b in (0, 1):
+            weights(b)
+        for b in (2, 3):
+            exponentials(b)
+        for r in (2, 3):
+            val_words[r] = tile([P, P * PACK], BF16, "vals%d_words" % r)
+            gather_values(r, val_words[r][:])
+        for b in (2, 3):
+            invert_sum(b)
+        for b in (0, 1):
+            w_q[b] = quantise("w%d" % b, w_words[b][:], P)
+        for b in (2, 3):
+            weights(b)
+
+        vals01_q = quantise("vals01", vals01_words[:], 2 * P)
+        vals_q = [(vals01_q, slice(0, P)), (vals01_q, slice(P, 2 * P))]
+        vals_q.extend((quantise("vals%d" % r, val_words[r][:], P), slice(0, P)) for r in (2, 3))
+        for b in (0, 1):
+            second_product(b)
+        inp_words = interleave("inp_words", inp_raw, X)
+        wg_q = quantise("wg", wg_words[:], E)
+        for b in (2, 3):
+            w_q[b] = quantise("w%d" % b, w_words[b][:], P)
+        for b in (2, 3):
+            second_product(b)
+        times_own(0)
+
+        inp_q = quantise("inp", inp_words[:], X)
+        g_ps = ps.tile([P, PACK, X], F32, name="g_ps", tag="misc", bufs=1)
+        for r in range(PACK):
+            product(g_ps[:, r, :], wg_q, slice(r * P, (r + 1) * P), inp_q)
+        g_tanh = tile([P, PACK, X], F32, "g_tanh")
+        nc.scalar.activation(g_tanh[:], g_ps[:], ACT.Tanh, scale=0.5)
+        gate = tile([P, PACK, X], F32, "gate")
+        nc.scalar.activation(gate[:], g_tanh[:], ACT.Copy, scale=0.5, bias=0.5)
+
+        for b in range(LAST):
+            add_halves(b)
+            times_own(b + 1)
+        for b in (0, 1, LAST, LAST - 1):
+            sum_places(b)
+
+        x_halves = [slice(0, X // 2), slice(X // 2, X)]
+        for cols in x_halves:
+            nc.vector.tensor_tensor(y[:, :, cols], sums[:, :, cols], gate[:, :, cols], ALU.mult)
+        y_by_place = y_words[:].rearrange("p (x r) -> p x r", r=PACK)
+        for copy, cols in zip((nc.scalar.copy, nc.vector.tensor_copy), x_halves):
+            copy(y_by_place[:, cols, :], y[:, :, cols].rearrange("p r x -> p x r"))
         nc.scalar.dma_start(out_0.rearrange("(p r) x -> p r x", r=PACK), y[:])
-        y_codes, y_scales = quantise("y", y_w[:], X)
+        y_codes, y_scales = quantise("y", y_words[:], X)
         nc.sync.dma_start(out_1[0].rearrange("p c r -> p (c r)").bitcast(I32), y_codes[:].bitcast(I32))
         for g in range(4):
-            eng = nc.scalar if g % 2 else nc.sync
-            eng.dma_start(out_2[0, 4 * g:4 * g + 4, :].bitcast(I32), y_scales[32 * g:32 * g + 4, :].bitcast(I32))
+            queue = nc.scalar if g % 2 else nc.sync
+            queue.dma_start(out_2[0, 4 * g:4 * g + 4, :].bitcast(I32), y_scales[32 * g:32 * g + 4, :].bitcast(I32))

from contextlib import ExitStack

import concourse.mybir as mybir
from concourse.masks import make_identity

D, T, I, Q, X, E, K = 512, 1024, 512, 512, 64, 512, 512
FLOPS = 2 * D * Q * I + 2 * I * E * Q + 2 * K * E * X

F32 = mybir.dt.float32
BF16 = mybir.dt.bfloat16
I32 = mybir.dt.int32
U32 = mybir.dt.uint32
U16 = mybir.dt.uint16
U8 = mybir.dt.uint8
FP8X4 = mybir.dt.float8_e4m3fn_x4
ALU = mybir.AluOpType
ACT = mybir.ActivationFunctionType
AXIS = mybir.AxisListType

P = 128
PACK = 4
HEADS = 8
LINE = 4
TILES = Q // P
PLACES = P // HEADS
WG_PIECES = 4
LAST = TILES - 1


def tile_attend_ownlists_gate_pl_kernel(tc, query, keys, size, vals, own, inp, wg, offs, out_0, out_1, out_2):
    nc = tc.nc
    with ExitStack() as ctx:
        sb = ctx.enter_context(tc.tile_pool(name="sb", bufs=1))
        ps = ctx.enter_context(tc.psum_pool(name="ps", bufs=1))

        reuses = {
            "vals_g0": "query_raw0",
            "vals_g1": "query_raw1",
            "vals_g2": "w0",
            "vals_g3": "w1",
            "vals01_codes": "w2",
            "wg_codes": "vals01_words",
            "inp_codes": "w3_words",
        }

        def tile(shape, dtype, name):
            return sb.tile(shape, dtype, name=name, tag=reuses.get(name, name), align_bytes=64)

        def load(shape, name, source):
            raw = tile(shape, F32, name)
            nc.sync.dma_start(raw[:], source)
            return raw

        def quantise(name, words, columns):
            codes = tile([P, columns], U32, name + "_codes")
            scales = tile([P, columns], U8, name + "_scales")
            nc.vector.quantize_mx(out=codes[:].bitcast(FP8X4), scales=scales[:], in_=words)
            return codes, scales

        def product(out, lhs, lhs_cols, rhs):
            nc.tensor.matmul_mx(out=out, lhsT=lhs[0][:, lhs_cols].bitcast(FP8X4), lhsT_scale=lhs[1][:, lhs_cols],
                                rhs=rhs[0][:].bitcast(FP8X4), rhs_scale=rhs[1][:], start=True, stop=True)

        def interleave(name, planes, columns):
            words = tile([P, columns * PACK], BF16, name)
            nc.scalar.copy(words[:].rearrange("p (c i t) -> p c t i", i=LINE, t=PACK),
                           planes[:].rearrange("p t (c i) -> p c t i", i=LINE))
            return words

        def turn(words, rows, bank):
            for u in range(2):
                nc.tensor.transpose(bank[:, u, :], rows[:].bitcast(F32)[:, u:I // 2:2], ident[:])
            nc.scalar.copy(words.bitcast(F32).rearrange("p (c u) -> p c u", u=2), bank[:].rearrange("p u c -> p c u"))

        keys_v = keys.rearrange("(p j) t -> j p t", j=PACK)
        vals_v = vals.rearrange("(p j) t -> j p t", j=PACK)
        query_v = query.rearrange("(p j) q -> p j q", j=PACK)
        offsets = sb.tile([P, I // 16], U16, name="offsets")
        key_planes = [load([P, T], "key_plane0", keys_v[0])]
        nc.sync.dma_start(offsets[:], offs)
        size_cols = load([P, PACK], "size_cols", size.rearrange("o (s t) -> s (o t)", t=PACK))
        key_planes.extend(load([P, T], "key_plane%d" % j, keys_v[j]) for j in range(1, PACK))
        query_raw, val_planes = [], []
        for h in range(2):
            query_raw.append(load([P, PACK, Q // 2], "query_raw%d" % h, query_v[:, :, h * (Q // 2):(h + 1) * (Q // 2)]))
            val_planes.append(load([P, T], "val_plane%d" % h, vals_v[h]))
        wg_raw = load([P, PACK, E], "wg_raw", wg.rearrange("(p j) e -> p j e", j=PACK))
        val_planes.extend(load([P, T], "val_plane%d" % j, vals_v[j]) for j in range(2, PACK))
        inp_raw = load([P, PACK, X], "inp_raw", inp.rearrange("(p j) x -> p j x", j=PACK))
        own_sb = load([P, PACK, Q], "own_sb", own.rearrange("(p j) q -> p j q", j=PACK))

        ident = sb.tile([P, P], F32, name="ident")
        make_identity(nc, ident[:])

        size_ps = ps.tile([P, PACK, P], F32, name="size_ps", tag="misc", bufs=1)
        for t in range(PACK):
            nc.tensor.transpose(size_ps[:, t, :], size_cols[:, t:t + 1].to_broadcast([P, P]), ident[:])
        size_row = tile([P, P, PACK], F32, "size_row")
        nc.scalar.activation(size_row[:], size_ps[:].rearrange("p t s -> p s t"), ACT.Copy)

        keys_g = tile([P, PACK, I], BF16, "keys_g")
        for j in range(PACK):
            nc.vector.tensor_copy(keys_g[:, j, :], key_planes[j][:].indirect(offsets[:]))
        keys_words = tile([P, I * PACK], BF16, "keys_words")
        keys_q = (tile([P, I], U32, "keys_codes"), tile([P, I], U8, "keys_scales"))
        by_pair = keys_words[:].rearrange("p (i u t) -> p u i t", u=2, t=2)
        nc.scalar.copy(by_pair[:, 0], keys_g[:, 0:2, :].rearrange("p t i -> p i t"))
        halves = [slice(0, I // 2), slice(I // 2, I)]
        for half in halves:
            nc.vector.tensor_copy(by_pair[:, 1, half], keys_g[:, 2:4, half].rearrange("p t i -> p i t"))
        for half in halves:
            nc.vector.quantize_mx(out=keys_q[0][:, half].bitcast(FP8X4), scales=keys_q[1][:, half],
                                  in_=keys_words[:, half.start * PACK:half.stop * PACK])

        sums = tile([P, PACK, X], F32, "sums")
        y = tile([P, PACK, X], F32, "y")
        y_words = tile([P, X * PACK], BF16, "y_words")
        scores, p_exp, p_sum, p_inv, w_words, w_q, val_words, o_ps, masked, halved = ({} for n in range(10))

        def score_pair(h, query_words):
            query_q = quantise("query%d" % h, query_words[:], Q // 2)
            for b in (2 * h, 2 * h + 1):
                scores[b] = ps.tile([P, I], F32, name="scores%d" % b, tag="big", bufs=4)
                product(scores[b][:], query_q, slice((b % 2) * P, (b % 2 + 1) * P), keys_q)

        def exponentials(b):
            neg_max = tile([P, 1], F32, "neg_max%d" % b)
            nc.vector.tensor_reduce(neg_max[:], scores[b][:], AXIS.X, ALU.max, negate=True)
            p_exp[b] = tile([P, I], F32, "p_exp%d" % b)
            p_sum[b] = tile([P, 1], F32, "p_sum%d" % b)
            nc.scalar.activation(p_exp[b][:], scores[b][:], ACT.Exp, bias=neg_max[:], accum_out=p_sum[b][:])

        def invert_sum(b):
            p_inv[b] = tile([P, 1], F32, "p_inv%d" % b)
            nc.vector.reciprocal(p_inv[b][:], p_sum[b][:])

        def weights(b):
            w = tile([P, I], BF16, "w%d" % b)
            nc.vector.scalar_tensor_tensor(w[:], p_exp[b][:], p_inv[b][:], size_row[:].rearrange("p s t -> p (s t)"),
                                           ALU.mult, ALU.mult)
            bank = ps.tile([P, 2, P], F32, name="w_ps%d" % b, tag="w_turn", bufs=2)
            w_words[b] = tile([P, P * PACK], BF16, "w%d_words" % b)
            turn(w_words[b][:], w, bank)

        def gather_values(r, words):
            vals_g = tile([P, I], BF16, "vals_g%d" % r)
            nc.vector.tensor_copy(vals_g[:], val_planes[r][:].indirect(offsets[:]))
            bank = ps.tile([P, 2, P], F32, name="v_ps%d" % r, tag="misc" if r % 2 else "v_turn", bufs=1)
            turn(words, vals_g, bank)

        def second_product(b):
            o_ps[b] = ps.tile([P, PACK, P], F32, name="o_ps%d" % b, tag="big", bufs=4)
            for r in range(PACK):
                product(o_ps[b][:, r, :], vals_q[r][0], vals_q[r][1], w_q[b])

        def times_own(b):
            own_b = own_sb[:, :, b * P:(b + 1) * P]
            masked[b] = tile([P, Q], F32, "masked%d" % b)
            if b == LAST:
                nc.vector.tensor_tensor(masked[b][:].rearrange("p (r q) -> p r q", r=PACK), o_ps[b][:], own_b, ALU.mult)
            else:
                nc.vector.tensor_tensor(masked[b][:].rearrange("p (h r x c) -> p r x h c", h=2, r=PACK, c=HEADS // 2),
                                        o_ps[b][:].rearrange("p r (x h c) -> p r x h c", h=2, c=HEADS // 2),
                                        own_b.rearrange("p r (x h c) -> p r x h c", h=2, c=HEADS // 2), ALU.mult)

        def add_halves(b):
            halved[b] = tile([P, Q // 2], F32, "halved%d" % b)
            nc.gpsimd.tensor_tensor(halved[b][:], masked[b][:, :Q // 2], masked[b][:, Q // 2:], ALU.add)

        def sum_places(b):
            terms = masked[b] if b == LAST else halved[b]
            nc.vector.tensor_reduce(sums[:, :, b * PLACES:(b + 1) * PLACES],
                                    terms[:].rearrange("p (r x c) -> p r x c", r=PACK, x=PLACES), AXIS.X, ALU.add)

        vals01_words = tile([P, 2 * P * PACK], BF16, "vals01_words")
        score_pair(0, interleave("query_words0", query_raw[0], Q // 2))
        gather_values(0, vals01_words[:, :P * PACK])
        query_words1 = interleave("query_words1", query_raw[1], Q // 2)
        for b in (0, 1):
            exponentials(b)
        score_pair(1, query_words1)
        gather_values(1, vals01_words[:, P * PACK:])
        for b in (0, 1):
            invert_sum(b)

        wg_words = tile([P, E * PACK], BF16, "wg_words")
        piece = P // WG_PIECES
        for c in range(WG_PIECES):
            nc.scalar.copy(wg_words[:].rearrange("p (r m t) -> p m t r", r=PACK, t=PACK)[:, c * piece:(c + 1) * piece],
                           wg_raw[:].rearrange("p t (m r) -> p m t r", r=PACK)[:, c * piece:(c + 1) * piece])

        for b in (0, 1):
            weights(b)
        for b in (2, 3):
            exponentials(b)
        for r in (2, 3):
            val_words[r] = tile([P, P * PACK], BF16, "vals%d_words" % r)
            gather_values(r, val_words[r][:])
        for b in (2, 3):
            invert_sum(b)
        for b in (0, 1):
            w_q[b] = quantise("w%d" % b, w_words[b][:], P)
        for b in (2, 3):
            weights(b)

        vals01_q = quantise("vals01", vals01_words[:], 2 * P)
        vals_q = [(vals01_q, slice(0, P)), (vals01_q, slice(P, 2 * P))]
        vals_q.extend((quantise("vals%d" % r, val_words[r][:], P), slice(0, P)) for r in (2, 3))
        for b in (0, 1):
            second_product(b)
        inp_words = interleave("inp_words", inp_raw, X)
        wg_q = quantise("wg", wg_words[:], E)
        for b in (2, 3):
            w_q[b] = quantise("w%d" % b, w_words[b][:], P)
        for b in (2, 3):
            second_product(b)
        times_own(0)

        inp_q = quantise("inp", inp_words[:], X)
        g_ps = ps.tile([P, PACK, X], F32, name="g_ps", tag="misc", bufs=1)
        for r in range(PACK):
            product(g_ps[:, r, :], wg_q, slice(r * P, (r + 1) * P), inp_q)
        g_tanh = tile([P, PACK, X], F32, "g_tanh")
        nc.scalar.activation(g_tanh[:], g_ps[:], ACT.Tanh, scale=0.5)
        gate = tile([P, PACK, X], F32, "gate")
        nc.scalar.activation(gate[:], g_tanh[:], ACT.Copy, scale=0.5, bias=0.5)

        for b in range(LAST):
            add_halves(b)
            times_own(b + 1)
        for b in (0, 1, LAST, LAST - 1):
            sum_places(b)

        x_halves = [slice(0, X // 2), slice(X // 2, X)]
        for cols in x_halves:
            nc.vector.tensor_tensor(y[:, :, cols], sums[:, :, cols], gate[:, :, cols], ALU.mult)
        y_by_place = y_words[:].rearrange("p (x r) -> p x r", r=PACK)
        for copy, cols in zip((nc.scalar.copy, nc.vector.tensor_copy), x_halves):
            copy(y_by_place[:, cols, :], y[:, :, cols].rearrange("p r x -> p x r"))
        nc.scalar.dma_start(out_0.rearrange("(p r) x -> p r x", r=PACK), y[:])
        y_codes, y_scales = quantise("y", y_words[:], X)
        nc.sync.dma_start(out_1[0].rearrange("p c r -> p (c r)").bitcast(I32), y_codes[:].bitcast(I32))
        for g in range(4):
            queue = nc.scalar if g % 2 else nc.sync
            queue.dma_start(out_2[0, 4 * g:4 * g + 4, :].bitcast(I32), y_scales[32 * g:32 * g + 4, :].bitcast(I32))
